import numpy as np
import ml_dtypes


def mxq(x, axis, fmt="e4m3"):
    dtype, down = {"e4m3": (ml_dtypes.float8_e4m3fn, 7), "e5m2": (ml_dtypes.float8_e5m2, 14)}[fmt]
    v = np.moveaxis(np.asarray(x, np.float32).astype(ml_dtypes.bfloat16).astype(np.float64), axis, -1)
    blocks = v.reshape(v.shape[:-1] + (-1, 32))
    amax = np.abs(blocks).max(-1, keepdims=True)
    byte = np.maximum(np.where(amax > 0, np.frexp(amax)[1] - 1 + 127, 0) - down, 1)
    scale = np.exp2(byte - 127.0)
    codes = (blocks / scale).astype(np.float32).astype(dtype).astype(np.float64)
    return np.moveaxis((codes * scale).reshape(v.shape), -1, axis)


WIDE = False


def mx_kscale(k):
    if not WIDE:
        return np.ones(k)
    levels = np.array([10, -10, 5, -5, 0])
    if k % 512:
        return np.exp2(np.random.permutation(np.resize(levels, k // 32))).repeat(32)
    a = np.empty((k // 512, 16))
    for p in range(k // 512):
        a[p, :8] = np.random.permutation(np.resize(levels, 8))
        for g in range(8):
            far = levels[np.abs(levels - a[p, g]) >= 10]
            a[p, g + 8] = far[np.random.randint(len(far))]
    return np.exp2(a.ravel()).repeat(32)


BF16 = ml_dtypes.bfloat16


def bf(x):
    return np.asarray(x, np.float32).astype(BF16)


def f64(x):
    return np.asarray(x).astype(np.float64)


E2M1 = np.array([0.0, 0.5, 1.0, 1.5, 2.0, 3.0, 4.0, 6.0, -0.0, -0.5, -1.0, -1.5, -2.0, -3.0, -4.0, -6.0])


def pack_weight(w, fmt):
    k, n = w.shape
    w = f64(bf(w)).reshape(k // 32, 32, n)
    amax = np.abs(w).max(1)
    if fmt == "e4m3":
        byte = np.frexp(amax)[1] - 1 + 127 - 7
    else:
        mant, ex = np.frexp(amax / 6.0)
        byte = np.where(mant > 0.5, ex, ex - 1) + 127
    byte = np.clip(np.where(amax > 0, byte, 1), 1, 254)
    scaled = (w * np.exp2(127.0 - byte)[:, None, :]).reshape(k, n).astype(np.float32)
    by_word = np.ascontiguousarray(scaled.reshape(k // 512, 128, 4, n).transpose(0, 1, 3, 2))
    if fmt == "e4m3":
        words = by_word.astype(ml_dtypes.float8_e4m3fn).view(np.uint8)
    else:
        c = by_word.astype(ml_dtypes.float4_e2m1fn).view(np.uint8) & 0xF
        words = c[..., 0::2] | (c[..., 1::2] << 4)
    return np.ascontiguousarray(words), np.ascontiguousarray(byte.astype(np.uint8).reshape(k // 512, 16, n))


def unpack_weight(words, scales, fmt):
    g, p, n, _ = words.shape
    if fmt == "e4m3":
        vals = np.ascontiguousarray(words).view(ml_dtypes.float8_e4m3fn).astype(np.float64)
    else:
        nib = np.empty((g, p, n, 4), np.uint8)
        nib[..., 0::2] = words & 0xF
        nib[..., 1::2] = words >> 4
        vals = E2M1[nib]
    vals = vals * np.repeat(np.exp2(scales.astype(np.float64) - 127.0), 8, axis=1)[..., None]
    return vals.transpose(0, 1, 3, 2).reshape(g * 512, n)
def pack4(w):
    words, scales = pack_weight(w, "e2m1")
    return words.reshape(words.shape[0], 128, -1), scales


def unpack4(words, scales):
    return unpack_weight(words.reshape(words.shape[0], 128, -1, 2), scales, "e2m1")


E4M3FN = np.array([(-1.0 if i & 128 else 1.0) * ((1.0 + (i & 7) / 8.0) * 2.0 ** (((i >> 3) & 15) - 7) if i & 120 else (i & 7) * 2.0 ** -9) for i in range(256)])


def e4m3fn_bytes(y):
    return np.clip(np.asarray(y, np.float64), -448.0, 448.0).astype(np.float32).astype(ml_dtypes.float8_e4m3fn).view(np.uint8)


def e4m3fn_values(b):
    return E4M3FN[b]


NQ, LQ, ND, LD, D, V = 128, 4, 256, 8, 512, 1024


def term_weights(x, w, b):
    logits = mxq(x, 2, "e4m3") @ w
    pooled = np.max(logits, axis=1)
    return np.log(1.0 + np.maximum(pooled + b, 0.0))


def centre_and_scale(r, g):
    return (r - np.mean(r, axis=0, keepdims=True)) * g


def draw0():
    sq, sd, t = mx_kscale(D), mx_kscale(D), mx_kscale(V)
    xq = bf(np.random.standard_normal((NQ, LQ, D)) * sq)
    xd = bf(np.random.standard_normal((ND, LD, D)) * sd)
    wq_words, wq_scales = pack4(np.random.standard_normal((D, V)) / np.sqrt(D) / sq[:, None])
    wd_words, wd_scales = pack4(np.random.standard_normal((D, V)) / np.sqrt(D) / sd[:, None])
    return {
        "xq": xq,
        "xd": xd,
        "wq_words": wq_words,
        "wq_scales": wq_scales,
        "wd_words": wd_words,
        "wd_scales": wd_scales,
        "b": bf(-1.0 + 0.5 * np.random.standard_normal(V)),
        "gq": bf((1.0 + 0.1 * np.random.standard_normal(V)) * t),
        "gd": bf((1.0 + 0.1 * np.random.standard_normal(V)) / t),
    }


def core(xq, xd, wq_words, wq_scales, wd_words, wd_scales, b, gq, gd):
    rq = term_weights(f64(xq), unpack4(wq_words, wq_scales), f64(b))
    rd = term_weights(f64(xd), unpack4(wd_words, wd_scales), f64(b))
    cq = centre_and_scale(rq, f64(gq))
    cd = centre_and_scale(rd, f64(gd))
    return mxq(cq, 1, "e4m3") @ mxq(cd, 1, "e4m3").T


def setup_inputs():
    drawn = draw0()
    full = np.asarray(drawn['xd']).astype(np.float64)
    scale = (np.abs(full).reshape(256, 8, 4, 128).max(axis=(3,)) / 448.0).astype(np.float32)
    given = {}
    for key, value in drawn.items():
        if key == 'xd':
            given['xd_bytes'] = e4m3fn_bytes(full / np.repeat(scale.astype(np.float64), 128, axis=2))
            given['xd_scale'] = scale
        else:
            given[key] = value
    return given


def reference(xq, xd_bytes, xd_scale, wq_words, wq_scales, wd_words, wd_scales, b, gq, gd):
    return core(xq, e4m3fn_values(xd_bytes) * np.repeat(xd_scale.astype(np.float64), 128, axis=2), wq_words, wq_scales, wd_words, wd_scales, b, gq, gd)

@@ -1,0 +1,420 @@
+import concourse.mybir as mybir
+from concourse.masks import make_identity
+from contextlib import ExitStack
+
+F32 = mybir.dt.float32
+BF16 = mybir.dt.bfloat16
+I32 = mybir.dt.int32
+U32 = mybir.dt.uint32
+U8 = mybir.dt.uint8
+E4M3 = mybir.dt.float8_e4m3fn
+E4M3X4 = mybir.dt.float8_e4m3fn_x4
+E2M1X4 = mybir.dt.float4_e2m1fn_x4
+ACT = mybir.ActivationFunctionType
+ALU = mybir.AluOpType
+AX = mybir.AxisListType
+
+P = 128
+NQ, LQ, ND, LD, D, V = 128, 4, 256, 8, 512, 1024
+VT = V // P
+BIG = 3.0e38
+FLOPS = 2 * D * V * (NQ * LQ + ND * LD) + 2 * V * NQ * ND
+
+
+def tile_efficientspladecentredscores_d1p_kernel(
+    tc, xq, xd_bytes, xd_scale, wq_words, wq_scales, wd_words, wd_scales, b, gq, gd, out
+):
+    nc = tc.nc
+    with ExitStack() as ctx:
+        keep = ctx.enter_context(tc.tile_pool(name="keep", bufs=1))
+        psum = ctx.enter_context(tc.psum_pool(name="psum", bufs=1))
+
+        xq_rows = xq.rearrange("n l d -> (n l) d").rearrange("(c p i) d -> c p (i d)", c=2, i=2)
+        xd_rows = xd_bytes.rearrange("n l d -> (n l) d").rearrange("(c p i) d -> c p (i d)", c=4, i=4)
+        xs_rows = xd_scale.rearrange("n l j -> (n l) j").rearrange("(c p i) j -> p c (i j)", c=4, i=4)
+
+        ctx.enter_context(tc.manual_schedule())
+
+        ones = keep.tile([P, 1], F32, name="ones", align_bytes=64)
+        nc.vector.memset(ones[:], 1.0)
+        ws_raw = [keep.tile([P, V], U8, name="ws_raw%d" % s, align_bytes=64) for s in range(2)]
+        vrows = keep.tile([P, P], BF16, name="vrows", align_bytes=64)
+        ident = keep.tile([P, P], F32, name="ident", align_bytes=64)
+        for s in range(2):
+            nc.vector.memset(ws_raw[s][:].bitcast(I32), 0)
+        nc.vector.memset(vrows[:], 0.0)
+        make_identity(nc, ident[:])
+
+        xw_q = [keep.tile([P, 2 * D], BF16, name="xw_q%d" % c, align_bytes=64) for c in range(2)]
+        xb = [keep.tile([P, 4 * D], U8, name="xb%d" % c, align_bytes=64) for c in range(4)]
+        xs = keep.tile([P, 4, 16], F32, name="xs", align_bytes=64)
+        ww_raw = [keep.tile([P, 2 * V], U8, name="ww_raw%d" % s, align_bytes=64) for s in range(2)]
+        words = (wq_words, wd_words)
+        scales = (wq_scales, wd_scales)
+
+        def load_words(s):
+            nc.sync.dma_start(out=ww_raw[s][:].bitcast(I32), in_=words[s][0].bitcast(I32))
+
+        def load_scales(s, eng):
+            for q in range(4):
+                eng.dma_start(
+                    out=ws_raw[s][32 * q : 32 * q + 4, :].bitcast(I32),
+                    in_=scales[s][0, 4 * q : 4 * q + 4, :].bitcast(I32),
+                )
+
+        nc.sync.dma_start(out=xw_q[0][:], in_=xq_rows[0])
+        load_words(0)
+        load_scales(0, nc.scalar)
+        warm = keep.tile([P, 1], F32, name="warm", align_bytes=64)
+        nc.scalar.activation(out=warm[:], in_=ones[:], func=ACT.Ln)
+        nc.sync.dma_start(out=xb[0][:], in_=xd_rows[0])
+        nc.gpsimd.dma_start(out=xs[:], in_=xs_rows)
+        nc.sync.dma_start(out=xw_q[1][:], in_=xq_rows[1])
+        nc.sync.dma_start(out=xb[1][:], in_=xd_rows[1])
+        load_words(1)
+        load_scales(1, nc.sync)
+        nc.sync.dma_start(out=xb[2][:], in_=xd_rows[2])
+        nc.sync.dma_start(out=xb[3][:], in_=xd_rows[3])
+        for i, vec in enumerate((b, gq, gd)):
+            halves = vec.rearrange("(g q j r) -> g j q r", g=2, q=16, j=4)
+            for g in range(2):
+                r0 = 8 * i + 4 * g
+                nc.sync.dma_start(
+                    out=vrows[r0 : r0 + 4, :].rearrange("j (q r) -> j q r", q=16), in_=halves[g]
+                )
+        ww = [keep.tile([P, 2 * V], U8, name="ww%d" % s, align_bytes=64) for s in range(2)]
+        ws = [keep.tile([P, V], U8, name="ws%d" % s, align_bytes=64) for s in range(2)]
+
+        def permute(s, g, eng):
+            for dst, src, n in ((ww[s], ww_raw[s], 4), (ws[s], ws_raw[s], 2)):
+                cols = slice(64 * n * g, 64 * n * (g + 1))
+                eng.tensor_copy(
+                    out=dst[:].bitcast(I32)[:, cols].rearrange("p (j q s) -> p j q s", j=4, q=16),
+                    in_=src[:].bitcast(I32)[:, cols].rearrange("p (q j s) -> p j q s", j=4, q=16),
+                )
+
+        chunks = [("q", 0), ("q", 1), ("d", 0), ("d", 1), ("d", 2), ("d", 3)]
+        tiles_of = [2, 2, 4, 4, 4, 4]
+        xw = list(xw_q) + [keep.tile([P, 4 * D], BF16, name="xw_d%d" % c, align_bytes=64) for c in range(4)]
+        xg = [keep.tile([P, 4 * P * tiles_of[n]], BF16, name="xg%d" % n, align_bytes=64) for n in range(6)]
+        xc = [keep.tile([P, P * tiles_of[n]], U32, name="xc%d" % n, align_bytes=64) for n in range(6)]
+        xcs = [keep.tile([P, P * tiles_of[n]], U8, name="xcs%d" % n, align_bytes=64) for n in range(6)]
+
+        def widen(n, lo, hi):
+            c = chunks[n][1]
+            for k in range(lo, hi):
+                cols = slice(P * k, P * (k + 1))
+                nc.scalar.activation(
+                    out=xw[n][:, cols], in_=xb[c][:, cols].bitcast(E4M3), func=ACT.Copy, scale=xs[:, c, k : k + 1]
+                )
+
+        def turn(n, h, eng):
+            tp = psum.tile([P, 2, 2, P], F32, name="tp", tag="tp", bufs=2)
+            pairs = xw[n][:].bitcast(F32)
+            for i in range(2):
+                for u in range(2):
+                    c0 = 256 * (2 * h + i)
+                    nc.tensor.transpose(tp[:, i, u, :], pairs[:, c0 + u : c0 + 256 : 2], ident[:])
+            dst = xg[n][:].bitcast(F32)[:, 512 * h : 512 * (h + 1)].rearrange("p (i r u) -> p i r u", i=2, u=2)
+            src = tp[:].rearrange("p i u r -> p i r u")
+            if eng == "v":
+                nc.vector.tensor_copy(out=dst, in_=src)
+            else:
+                nc.scalar.copy(out=dst, in_=src)
+
+        def quantize(n):
+            nc.vector.quantize_mx(out=xc[n][:].bitcast(E4M3X4), scales=xcs[n][:], in_=xg[n][:])
+
+        pooled = {
+            "q": keep.tile([P, VT, NQ], F32, name="pooled_q", align_bytes=64),
+            "d": keep.tile([P, VT, ND], F32, name="pooled_d", align_bytes=64),
+        }
+        banks = {}
+
+        def scores(n, vt):
+            side = 0 if chunks[n][0] == "q" else 1
+            width = P * tiles_of[n]
+            mm = psum.tile([P, 512], F32, name="mm", tag="mm", bufs=6)
+            nc.tensor.matmul_mx(
+                out=mm[:, :width],
+                lhsT=ww[side][:, 2 * P * vt : 2 * P * (vt + 1)].bitcast(E2M1X4),
+                lhsT_scale=ws[side][:, P * vt : P * (vt + 1)],
+                rhs=xc[n][:].bitcast(E4M3X4),
+                rhs_scale=xcs[n][:],
+                start=True,
+                stop=True,
+            )
+            banks[n, vt] = mm
+
+        def pool(n, vt):
+            kind, c = chunks[n]
+            width = P * tiles_of[n]
+            mm = banks.pop((n, vt))
+            nc.vector.tensor_reduce(
+                out=pooled[kind][:, vt, 64 * c : 64 * (c + 1)],
+                in_=mm[:, :width].rearrange("p (i d two) -> p d i two", i=tiles_of[n], two=2),
+                axis=AX.XY,
+                op=ALU.max,
+            )
+
+        vcols = keep.tile([P, 24], F32, name="vcols", align_bytes=64)
+        nb = keep.tile([P, VT], F32, name="nb", align_bytes=64)
+        b1 = keep.tile([P, VT], F32, name="b1", align_bytes=64)
+        gneg = keep.tile([P, 2 * VT], F32, name="gneg", align_bytes=64)
+        vrows_f = keep.tile([P, P], F32, name="vrows_f", align_bytes=64)
+
+        def vector_columns():
+            tp = psum.tile([P, P], F32, name="tpv", tag="tp", bufs=2)
+            nc.tensor.transpose(tp[:], vrows_f[:], ident[:])
+            nc.scalar.copy(out=vcols[:], in_=tp[:, :24])
+            nc.gpsimd.tensor_scalar(out=nb[:], in0=vcols[:, 0:VT], scalar1=-1.0, scalar2=0.0, op0=ALU.mult, op1=ALU.add)
+            nc.gpsimd.tensor_scalar(out=b1[:], in0=vcols[:, 0:VT], scalar1=1.0, scalar2=1.0, op0=ALU.mult, op1=ALU.add)
+
+        logs = {
+            "q": keep.tile([P, VT, NQ], F32, name="logs_q", align_bytes=64),
+            "d": keep.tile([P, VT, ND], F32, name="logs_d", align_bytes=64),
+        }
+        sums = {
+            "q": keep.tile([P, VT], F32, name="sums_q", align_bytes=64),
+            "d": keep.tile([P, VT], F32, name="sums_d", align_bytes=64),
+            "d2": keep.tile([P, 1], F32, name="sums_d2", align_bytes=64),
+        }
+        offs = {
+            "q": keep.tile([P, VT], F32, name="off_q", align_bytes=64),
+            "d": keep.tile([P, VT], F32, name="off_d", align_bytes=64),
+        }
+        off_part = keep.tile([P, 1], F32, name="off_part", align_bytes=64)
+
+        def negative_gains():
+            for k, count in enumerate((NQ, ND)):
+                cols = slice(VT * k, VT * (k + 1))
+                nc.gpsimd.tensor_scalar(
+                    out=gneg[:, cols], in0=vcols[:, VT + VT * k : 2 * VT + VT * k], scalar1=-1.0 / count, scalar2=0.0, op0=ALU.mult, op1=ALU.add
+                )
+
+        def clip(eng, kind, vt, lo, hi):
+            x = pooled[kind][:, vt, lo:hi]
+            eng.tensor_scalar(out=x, in0=x, scalar1=BIG, scalar2=nb[:, vt : vt + 1], op0=ALU.min, op1=ALU.max)
+
+        def log(kind, vt, lo, hi, acc):
+            nc.scalar.activation(
+                out=logs[kind][:, vt, lo:hi], in_=pooled[kind][:, vt, lo:hi], func=ACT.Ln, bias=b1[:, vt : vt + 1], accum_out=acc
+            )
+
+        cg = {
+            "q": [keep.tile([P, NQ, 4], BF16, name="cg_q%d" % g, align_bytes=64) for g in range(2)],
+            "d": [keep.tile([P, ND, 4], BF16, name="cg_d%d" % g, align_bytes=64) for g in range(2)],
+        }
+        cc = {
+            "q": keep.tile([P, 2, NQ], U32, name="cc_q", align_bytes=64),
+            "d": keep.tile([P, 2, ND], U32, name="cc_d", align_bytes=64),
+        }
+        ccs = {
+            "q": keep.tile([P, 2, NQ], U8, name="ccs_q", align_bytes=64),
+            "d": keep.tile([P, 2, ND], U8, name="ccs_d", align_bytes=64),
+        }
+
+        def shift(kind, vt):
+            base = 0 if kind == "q" else VT
+            nc.scalar.activation(
+                out=offs[kind][:, vt : vt + 1],
+                in_=sums[kind][:, vt : vt + 1],
+                func=ACT.Copy,
+                scale=gneg[:, base + vt : base + vt + 1],
+            )
+
+        def shift_q(g):
+            cols = slice(4 * g, 4 * g + 4)
+            nc.gpsimd.tensor_tensor(out=offs["q"][:, cols], in0=sums["q"][:, cols], in1=gneg[:, cols], op=ALU.mult)
+
+        def relu_log(kind, vt, lo, hi, acc):
+            x = pooled[kind][:, vt, lo:hi]
+            nc.scalar.activation(out=x, in_=x, func=ACT.Relu, bias=vcols[:, vt : vt + 1])
+            nc.scalar.activation(out=logs[kind][:, vt, lo:hi], in_=x, func=ACT.Ln, bias=ones[:], accum_out=acc)
+
+        def centre_g(kind, vt):
+            g, j = vt // 4, vt % 4
+            gain = (8 if kind == "q" else 16) + vt
+            nc.gpsimd.tensor_scalar(
+                out=cg[kind][g][:, :, j],
+                in0=logs[kind][:, vt, :],
+                scalar1=vcols[:, gain : gain + 1],
+                scalar2=offs[kind][:, vt : vt + 1],
+                op0=ALU.mult,
+                op1=ALU.add,
+            )
+
+        def centre_s(kind, vt):
+            g, j = vt // 4, vt % 4
+            gain = (8 if kind == "q" else 16) + vt
+            nc.scalar.activation(
+                out=cg[kind][g][:, :, j],
+                in_=logs[kind][:, vt, :],
+                func=ACT.Identity,
+                scale=vcols[:, gain : gain + 1],
+                bias=offs[kind][:, vt : vt + 1],
+            )
+
+        def centre_v(kind, vt):
+            g, j = vt // 4, vt % 4
+            gain = (8 if kind == "q" else 16) + vt
+            nc.vector.tensor_scalar(
+                out=cg[kind][g][:, :, j],
+                in0=logs[kind][:, vt, :],
+                scalar1=vcols[:, gain : gain + 1],
+                scalar2=offs[kind][:, vt : vt + 1],
+                op0=ALU.mult,
+                op1=ALU.add,
+            )
+
+        def quantize_centred(kind, g):
+            nc.vector.quantize_mx(
+                out=cc[kind][:, g, :].bitcast(E4M3X4),
+                scales=ccs[kind][:, g, :],
+                in_=cg[kind][g][:].rearrange("p d j -> p (d j)"),
+            )
+
+        permute(0, 0, nc.vector)
+        turn(0, 0, "v")
+        quantize(0)
+        permute(0, 1, nc.vector)
+        if -1 < 0:
+            turn(1, 0, "v")
+        permute(1, 0, nc.gpsimd)
+        permute(1, 1, nc.gpsimd)
+        widen(2, 0, 16)
+
+        order = [(n, vt) for n in range(4) for vt in range(VT)]
+        LEAD = 0
+        last = (0, 4, 1, 5, 2, 3, 6, 7)
+        order += [(4, vt) for vt in last[:LEAD]]
+        for k, vt in enumerate(last):
+            if k + LEAD < VT:
+                order.append((4, last[k + LEAD]))
+            order.append((5, vt))
+        AHEAD = 3
+
+        late = []
+
+        def finish_shift():
+            if late:
+                shift("d", late[0])
+                if late[0] < 4:
+                    centre_g("d", late[0])
+
+        def finish_centre():
+            if late:
+                k = late.pop()
+                if 4 <= k < 6:
+                    centre_s("d", k)
+
+        def query_logs(lo, hi):
+            for k in range(lo, hi):
+                log("q", k, 0, NQ, sums["q"][:, k : k + 1])
+                if k % 4 == 3:
+                    shift_q(k // 4)
+                    for m in range(k - 3, k + 1):
+                        if m < 4:
+                            centre_g("q", m)
+
+        for i in range(AHEAD):
+            scores(*order[i])
+        for i, (n, vt) in enumerate(order):
+            if i + AHEAD < len(order):
+                scores(*order[i + AHEAD])
+            pool(n, vt)
+            if i == -1:
+                turn(1, 0, "v")
+            if i == 0:
+                quantize(1)
+            if i == 6:
+                nc.vector.tensor_copy(out=vrows_f[:], in_=vrows[:])
+            if i == 3:
+                turn(2, 0, "s")
+                turn(2, 1, "s")
+                widen(3, 0, 16)
+            if i == 7:
+                vector_columns()
+            if 8 <= i < 16:
+                clip(nc.gpsimd, "q", i - 8, 0, NQ)
+                if i == 15:
+                    negative_gains()
+            if i == 9:
+                quantize(2)
+            if i == 13:
+                turn(3, 0, "s")
+                turn(3, 1, "s")
+                widen(4, 0, 16)
+            if i == 16:
+                query_logs(0, 4)
+            if i == 19:
+                quantize(3)
+            if i == 19:
+                turn(4, 0, "s")
+                turn(4, 1, "s")
+                widen(5, 0, 16)
+                query_logs(4, 4)
+            if i == 28:
+                quantize(4)
+            if i == 27:
+                turn(5, 0, "s")
+                turn(5, 1, "s")
+                query_logs(4, 8)
+                for m in range(4, 8):
+                    centre_s("q", m)
+            if i == 29:
+                quantize(5)
+            if n == 5 and vt < 7:
+                x = pooled["d"][:, vt, :]
+                if vt < 4:
+                    clip(nc.gpsimd, "d", vt, 0, ND)
+                elif vt < 4:
+                    clip(nc.vector, "d", vt, 0, ND)
+                finish_shift()
+                if vt >= 4:
+                    nc.scalar.activation(out=x, in_=x, func=ACT.Relu, bias=vcols[:, vt : vt + 1])
+                finish_centre()
+                nc.scalar.activation(
+                    out=logs["d"][:, vt, :],
+                    in_=x,
+                    func=ACT.Ln,
+                    bias=(b1[:, vt : vt + 1] if vt < 4 else ones[:]),
+                    accum_out=sums["d"][:, vt : vt + 1],
+                )
+                late.append(vt)
+            if i == 44:
+                quantize_centred("q", 0)
+                quantize_centred("q", 1)
+        x = pooled["d"][:, 7, 0:192]
+        nc.scalar.activation(out=x, in_=x, func=ACT.Relu, bias=vcols[:, 7:8])
+        finish_shift()
+        nc.scalar.activation(out=logs["d"][:, 7, 0:192], in_=x, func=ACT.Ln, bias=ones[:], accum_out=sums["d2"][:])
+        finish_centre()
+        x = pooled["d"][:, 7, 192:256]
+        nc.scalar.activation(out=x, in_=x, func=ACT.Relu, bias=vcols[:, 7:8])
+        nc.scalar.activation(out=off_part[:], in_=sums["d2"][:], func=ACT.Copy, scale=gneg[:, 15:16])
+        nc.scalar.activation(out=logs["d"][:, 7, 192:256], in_=x, func=ACT.Ln, bias=ones[:], accum_out=sums["d"][:, 7:8])
+        nc.scalar.activation(out=offs["d"][:, 7:8], in_=sums["d"][:, 7:8], func=ACT.Identity, scale=gneg[:, 15:16], bias=off_part[:])
+        centre_v("d", 6)
+        quantize_centred("d", 0)
+        centre_v("d", 7)
+        outs = [psum.tile([P, 512], F32, name="mm", tag="mm", bufs=6) for h in range(2)]
+        for g in range(2):
+            if g == 1:
+                quantize_centred("d", 1)
+            for h in range(2):
+                cols = slice(P * h, P * (h + 1))
+                nc.tensor.matmul_mx(
+                    out=outs[h][:, :P],
+                    lhsT=cc["q"][:, g, :].bitcast(E4M3X4),
+                    lhsT_scale=ccs["q"][:, g, :],
+                    rhs=cc["d"][:, g, cols].bitcast(E4M3X4),
+                    rhs_scale=ccs["d"][:, g, cols],
+                    start=(g == 0),
+                    stop=(g == 1),
+                )
+        res = [keep.tile([P, P], F32, name="res%d" % h, align_bytes=64) for h in range(2)]
+        nc.vector.tensor_copy(out=res[0][:], in_=outs[0][:, :P])
+        nc.sync.dma_start(out=out[:, :P], in_=res[0][:])
+        nc.scalar.copy(out=res[1][:], in_=outs[1][:, :P])
+        nc.scalar.dma_start(out=out[:, P:], in_=res[1][:])

@@ -30,8 +30,8 @@ def tile_efficientspladecentredscores_d1p_kernel(
         psum = ctx.enter_context(tc.psum_pool(name="psum", bufs=1))
 
         xq_rows = xq.rearrange("n l d -> (n l) d").rearrange("(c p i) d -> c p (i d)", c=2, i=2)
-        xd_rows = xd_bytes.rearrange("n l d -> (n l) d").rearrange("(c p i) d -> c p (i d)", c=4, i=4)
-        xs_rows = xd_scale.rearrange("n l j -> (n l) j").rearrange("(c p i) j -> p c (i j)", c=4, i=4)
+        xd_rows = xd_bytes.rearrange("n l d -> (n l) d").rearrange("(c e p i) d -> c p e (i d)", c=4, e=2, i=2)
+        xs_rows = xd_scale.rearrange("n l j -> (n l) j").rearrange("(c e p i) j -> c p e (i j)", c=4, e=2, i=2)
 
         ctx.enter_context(tc.manual_schedule())
 
@@ -47,7 +47,7 @@ def tile_efficientspladecentredscores_d1p_kernel(
 
         xw_q = [keep.tile([P, 2 * D], BF16, name="xw_q%d" % c, align_bytes=64) for c in range(2)]
         xb = [keep.tile([P, 4 * D], U8, name="xb%d" % c, align_bytes=64) for c in range(4)]
-        xs = keep.tile([P, 4, 16], F32, name="xs", align_bytes=64)
+        xs = [keep.tile([P, 16], F32, name="xs%d" % c, align_bytes=64) for c in range(4)]
         ww_raw = [keep.tile([P, 2 * V], U8, name="ww_raw%d" % s, align_bytes=64) for s in range(2)]
         words = (wq_words, wd_words)
         scales = (wq_scales, wd_scales)
@@ -67,14 +67,15 @@ def tile_efficientspladecentredscores_d1p_kernel(
         load_scales(0, nc.scalar)
         warm = keep.tile([P, 1], F32, name="warm", align_bytes=64)
         nc.scalar.activation(out=warm[:], in_=ones[:], func=ACT.Ln)
-        nc.sync.dma_start(out=xb[0][:], in_=xd_rows[0])
-        nc.gpsimd.dma_start(out=xs[:], in_=xs_rows)
+        nc.sync.dma_start(out=xb[0][:].rearrange("p (e k) -> p e k", e=2), in_=xd_rows[0])
+        for c in range(4):
+            nc.gpsimd.dma_start(out=xs[c][:].rearrange("p (e k) -> p e k", e=2), in_=xs_rows[c])
         nc.sync.dma_start(out=xw_q[1][:], in_=xq_rows[1])
-        nc.sync.dma_start(out=xb[1][:], in_=xd_rows[1])
+        nc.sync.dma_start(out=xb[1][:].rearrange("p (e k) -> p e k", e=2), in_=xd_rows[1])
         load_words(1)
         load_scales(1, nc.sync)
-        nc.sync.dma_start(out=xb[2][:], in_=xd_rows[2])
-        nc.sync.dma_start(out=xb[3][:], in_=xd_rows[3])
+        nc.sync.dma_start(out=xb[2][:].rearrange("p (e k) -> p e k", e=2), in_=xd_rows[2])
+        nc.sync.dma_start(out=xb[3][:].rearrange("p (e k) -> p e k", e=2), in_=xd_rows[3])
         for i, vec in enumerate((b, gq, gd)):
             halves = vec.rearrange("(g q j r) -> g j q r", g=2, q=16, j=4)
             for g in range(2):
@@ -105,7 +106,7 @@ def tile_efficientspladecentredscores_d1p_kernel(
             for k in range(lo, hi):
                 cols = slice(P * k, P * (k + 1))
                 nc.scalar.activation(
-                    out=xw[n][:, cols], in_=xb[c][:, cols].bitcast(E4M3), func=ACT.Copy, scale=xs[:, c, k : k + 1]
+                    out=xw[n][:, cols], in_=xb[c][:, cols].bitcast(E4M3), func=ACT.Copy, scale=xs[c][:, k : k + 1]
                 )
 
         def turn(n, h, eng):
@@ -150,9 +151,10 @@ def tile_efficientspladecentredscores_d1p_kernel(
             kind, c = chunks[n]
             width = P * tiles_of[n]
             mm = banks.pop((n, vt))
+            sub = tiles_of[n] // 2
             nc.vector.tensor_reduce(
-                out=pooled[kind][:, vt, 64 * c : 64 * (c + 1)],
-                in_=mm[:, :width].rearrange("p (i d two) -> p d i two", i=tiles_of[n], two=2),
+                out=pooled[kind][:, vt, 64 * c : 64 * (c + 1)].rearrange("p (e d) -> p e d", e=sub),
+                in_=mm[:, :width].rearrange("p (e i d l) -> p e d i l", e=sub, i=2, l=2 * sub),
                 axis=AX.XY,
                 op=ALU.max,
             )
@@ -183,7 +185,8 @@ def tile_efficientspladecentredscores_d1p_kernel(
             "q": keep.tile([P, VT], F32, name="off_q", align_bytes=64),
             "d": keep.tile([P, VT], F32, name="off_d", align_bytes=64),
         }
-        off_part = keep.tile([P, 1], F32, name="off_part", align_bytes=64)
+        off_g = keep.tile([P, VT], F32, name="off_g", align_bytes=64)
+        off_v = keep.tile([P, VT], F32, name="off_v", align_bytes=64)
 
         def negative_gains():
             for k, count in enumerate((NQ, ND)):
@@ -214,14 +217,21 @@ def tile_efficientspladecentredscores_d1p_kernel(
             "d": keep.tile([P, 2, ND], U8, name="ccs_d", align_bytes=64),
         }
 
-        def shift(kind, vt):
-            base = 0 if kind == "q" else VT
-            nc.scalar.activation(
-                out=offs[kind][:, vt : vt + 1],
-                in_=sums[kind][:, vt : vt + 1],
-                func=ACT.Copy,
-                scale=gneg[:, base + vt : base + vt + 1],
-            )
+        def shift(vt):
+            col = slice(vt, vt + 1)
+            gain = gneg[:, VT + vt : VT + vt + 1]
+            if vt < 0:
+                nc.gpsimd.tensor_scalar(out=off_g[:, col], in0=sums["d"][:, col], scalar1=gain, scalar2=0.0, op0=ALU.mult, op1=ALU.add)
+            elif vt < 6:
+                nc.scalar.activation(out=offs["d"][:, col], in_=sums["d"][:, col], func=ACT.Copy, scale=gain)
+            elif vt < 7:
+                nc.vector.tensor_scalar(out=off_v[:, col], in0=sums["d"][:, col], scalar1=gain, scalar2=0.0, op0=ALU.mult, op1=ALU.add)
+            else:
+                nc.vector.tensor_scalar(out=off_v[:, col], in0=sums["d"][:, col], scalar1=sums["d2"][:], scalar2=gain, op0=ALU.add, op1=ALU.mult)
+
+        def off(kind, vt):
+            t = offs[kind] if kind == "q" else (off_g if vt < 0 else (offs["d"] if vt < 6 else off_v))
+            return t[:, vt : vt + 1]
 
         def shift_q(g):
             cols = slice(4 * g, 4 * g + 4)
@@ -239,7 +249,7 @@ def tile_efficientspladecentredscores_d1p_kernel(
                 out=cg[kind][g][:, :, j],
                 in0=logs[kind][:, vt, :],
                 scalar1=vcols[:, gain : gain + 1],
-                scalar2=offs[kind][:, vt : vt + 1],
+                scalar2=off(kind, vt),
                 op0=ALU.mult,
                 op1=ALU.add,
             )
@@ -252,7 +262,7 @@ def tile_efficientspladecentredscores_d1p_kernel(
                 in_=logs[kind][:, vt, :],
                 func=ACT.Identity,
                 scale=vcols[:, gain : gain + 1],
-                bias=offs[kind][:, vt : vt + 1],
+                bias=off(kind, vt),
             )
 
         def centre_v(kind, vt):
@@ -262,7 +272,7 @@ def tile_efficientspladecentredscores_d1p_kernel(
                 out=cg[kind][g][:, :, j],
                 in0=logs[kind][:, vt, :],
                 scalar1=vcols[:, gain : gain + 1],
-                scalar2=offs[kind][:, vt : vt + 1],
+                scalar2=off(kind, vt),
                 op0=ALU.mult,
                 op1=ALU.add,
             )
@@ -274,14 +284,18 @@ def tile_efficientspladecentredscores_d1p_kernel(
                 in_=cg[kind][g][:].rearrange("p d j -> p (d j)"),
             )
 
+        idle = keep.tile([P, 512], BF16, name="idle", align_bytes=64)
+        nc.vector.memset(idle[:], 0.0)
+        wake = psum.tile([P, 512], F32, name="mm", tag="mm", bufs=6)
+        for k in range(4):
+            nc.tensor.matmul(wake[:], lhsT=idle[:, :P], rhs=idle[:], start=True, stop=True)
+
         permute(0, 0, nc.vector)
         turn(0, 0, "v")
         quantize(0)
         permute(0, 1, nc.vector)
         if -1 < 0:
             turn(1, 0, "v")
-        permute(1, 0, nc.gpsimd)
-        permute(1, 1, nc.gpsimd)
         widen(2, 0, 16)
 
         order = [(n, vt) for n in range(4) for vt in range(VT)]
@@ -292,13 +306,14 @@ def tile_efficientspladecentredscores_d1p_kernel(
             if k + LEAD < VT:
                 order.append((4, last[k + LEAD]))
             order.append((5, vt))
-        AHEAD = 3
+        AHEAD = 2
 
         late = []
 
         def finish_shift():
             if late:
-                shift("d", late[0])
+                if late[0] < 6:
+                    shift(late[0])
                 if late[0] < 4:
                     centre_g("d", late[0])
 
@@ -310,19 +325,30 @@ def tile_efficientspladecentredscores_d1p_kernel(
 
         def query_logs(lo, hi):
             for k in range(lo, hi):
-                log("q", k, 0, NQ, sums["q"][:, k : k + 1])
+                if 0 == 2:
+                    relu_log("q", k, 0, NQ, sums["q"][:, k : k + 1])
+                else:
+                    log("q", k, 0, NQ, sums["q"][:, k : k + 1])
                 if k % 4 == 3:
                     shift_q(k // 4)
                     for m in range(k - 3, k + 1):
-                        if m < 4:
+                        if m < 0:
                             centre_g("q", m)
 
+        GROUP = 2
+        pools = [order[k + GROUP - 1 - m] for k in range(0, len(order), GROUP) for m in range(GROUP)]
+        seen = set()
         for i in range(AHEAD):
             scores(*order[i])
-        for i, (n, vt) in enumerate(order):
+        for i, (n, vt) in enumerate(pools):
             if i + AHEAD < len(order):
                 scores(*order[i + AHEAD])
             pool(n, vt)
+            seen.add((n, vt))
+            if i == 4:
+                permute(1, 0, nc.vector)
+            if i == 3:
+                permute(1, 1, nc.vector)
             if i == -1:
                 turn(1, 0, "v")
             if i == 0:
@@ -336,37 +362,40 @@ def tile_efficientspladecentredscores_d1p_kernel(
             if i == 7:
                 vector_columns()
             if 8 <= i < 16:
-                clip(nc.gpsimd, "q", i - 8, 0, NQ)
+                if 0 == 0:
+                    clip(nc.gpsimd, "q", vt, 0, NQ)
+                elif 0 == 1:
+                    clip(nc.vector, "q", vt, 0, NQ)
                 if i == 15:
                     negative_gains()
-            if i == 9:
+            if i == 11:
                 quantize(2)
             if i == 13:
                 turn(3, 0, "s")
                 turn(3, 1, "s")
                 widen(4, 0, 16)
             if i == 16:
-                query_logs(0, 4)
-            if i == 19:
+                query_logs(0, 0)
+            if i == 17:
                 quantize(3)
-            if i == 19:
+            if i == 20:
                 turn(4, 0, "s")
                 turn(4, 1, "s")
                 widen(5, 0, 16)
-                query_logs(4, 4)
-            if i == 28:
+                query_logs(0, 0)
+            if i == 29:
                 quantize(4)
             if i == 27:
                 turn(5, 0, "s")
                 turn(5, 1, "s")
-                query_logs(4, 8)
-                for m in range(4, 8):
+                query_logs(0, 8)
+                for m in range(0, 8):
                     centre_s("q", m)
-            if i == 29:
+            if i == 28:
                 quantize(5)
-            if n == 5 and vt < 7:
+            if n >= 4 and vt < 7 and (4, vt) in seen and (5, vt) in seen:
                 x = pooled["d"][:, vt, :]
-                if vt < 4:
+                if vt < 3:
                     clip(nc.gpsimd, "d", vt, 0, ND)
                 elif vt < 4:
                     clip(nc.vector, "d", vt, 0, ND)
@@ -382,7 +411,7 @@ def tile_efficientspladecentredscores_d1p_kernel(
                     accum_out=sums["d"][:, vt : vt + 1],
                 )
                 late.append(vt)
-            if i == 44:
+            if i == 43:
                 quantize_centred("q", 0)
                 quantize_centred("q", 1)
         x = pooled["d"][:, 7, 0:192]
@@ -392,10 +421,10 @@ def tile_efficientspladecentredscores_d1p_kernel(
         finish_centre()
         x = pooled["d"][:, 7, 192:256]
         nc.scalar.activation(out=x, in_=x, func=ACT.Relu, bias=vcols[:, 7:8])
-        nc.scalar.activation(out=off_part[:], in_=sums["d2"][:], func=ACT.Copy, scale=gneg[:, 15:16])
         nc.scalar.activation(out=logs["d"][:, 7, 192:256], in_=x, func=ACT.Ln, bias=ones[:], accum_out=sums["d"][:, 7:8])
-        nc.scalar.activation(out=offs["d"][:, 7:8], in_=sums["d"][:, 7:8], func=ACT.Identity, scale=gneg[:, 15:16], bias=off_part[:])
+        shift(6)
         centre_v("d", 6)
+        shift(7)
         quantize_centred("d", 0)
         centre_v("d", 7)
         outs = [psum.tile([P, 512], F32, name="mm", tag="mm", bufs=6) for h in range(2)]

@@ -30,8 +30,8 @@ def tile_efficientspladecentredscores_d1p_kernel(
         psum = ctx.enter_context(tc.psum_pool(name="psum", bufs=1))
 
         xq_rows = xq.rearrange("n l d -> (n l) d").rearrange("(c p i) d -> c p (i d)", c=2, i=2)
-        xd_rows = xd_bytes.rearrange("n l d -> (n l) d").rearrange("(c e p i) d -> c p e (i d)", c=4, e=2, i=2)
-        xs_rows = xd_scale.rearrange("n l j -> (n l) j").rearrange("(c e p i) j -> c p e (i j)", c=4, e=2, i=2)
+        xd_rows = xd_bytes.rearrange("n l d -> (n l) d").rearrange("(c p i) d -> c p (i d)", c=4, i=4)
+        xs_rows = xd_scale.rearrange("n l j -> (n l) j").rearrange("(c p i) j -> p c (i j)", c=4, i=4)
 
         ctx.enter_context(tc.manual_schedule())
 
@@ -47,7 +47,7 @@ def tile_efficientspladecentredscores_d1p_kernel(
 
         xw_q = [keep.tile([P, 2 * D], BF16, name="xw_q%d" % c, align_bytes=64) for c in range(2)]
         xb = [keep.tile([P, 4 * D], U8, name="xb%d" % c, align_bytes=64) for c in range(4)]
-        xs = [keep.tile([P, 16], F32, name="xs%d" % c, align_bytes=64) for c in range(4)]
+        xs = keep.tile([P, 4, 16], F32, name="xs", align_bytes=64)
         ww_raw = [keep.tile([P, 2 * V], U8, name="ww_raw%d" % s, align_bytes=64) for s in range(2)]
         words = (wq_words, wd_words)
         scales = (wq_scales, wd_scales)
@@ -62,20 +62,20 @@ def tile_efficientspladecentredscores_d1p_kernel(
                     in_=scales[s][0, 4 * q : 4 * q + 4, :].bitcast(I32),
                 )
 
+        load_scales(0, nc.scalar)
         nc.sync.dma_start(out=xw_q[0][:], in_=xq_rows[0])
         load_words(0)
-        load_scales(0, nc.scalar)
         warm = keep.tile([P, 1], F32, name="warm", align_bytes=64)
         nc.scalar.activation(out=warm[:], in_=ones[:], func=ACT.Ln)
-        nc.sync.dma_start(out=xb[0][:].rearrange("p (e k) -> p e k", e=2), in_=xd_rows[0])
-        for c in range(4):
-            nc.gpsimd.dma_start(out=xs[c][:].rearrange("p (e k) -> p e k", e=2), in_=xs_rows[c])
+        nc.sync.dma_start(out=xb[0][:], in_=xd_rows[0])
+        nc.sync.dma_start(out=xs[:, 0, :], in_=xs_rows[:, 0, :])
         nc.sync.dma_start(out=xw_q[1][:], in_=xq_rows[1])
-        nc.sync.dma_start(out=xb[1][:].rearrange("p (e k) -> p e k", e=2), in_=xd_rows[1])
+        nc.sync.dma_start(out=xb[1][:], in_=xd_rows[1])
+        nc.sync.dma_start(out=xs[:, 1:, :], in_=xs_rows[:, 1:, :])
         load_words(1)
         load_scales(1, nc.sync)
-        nc.sync.dma_start(out=xb[2][:].rearrange("p (e k) -> p e k", e=2), in_=xd_rows[2])
-        nc.sync.dma_start(out=xb[3][:].rearrange("p (e k) -> p e k", e=2), in_=xd_rows[3])
+        nc.sync.dma_start(out=xb[2][:], in_=xd_rows[2])
+        nc.sync.dma_start(out=xb[3][:], in_=xd_rows[3])
         for i, vec in enumerate((b, gq, gd)):
             halves = vec.rearrange("(g q j r) -> g j q r", g=2, q=16, j=4)
             for g in range(2):
@@ -106,7 +106,7 @@ def tile_efficientspladecentredscores_d1p_kernel(
             for k in range(lo, hi):
                 cols = slice(P * k, P * (k + 1))
                 nc.scalar.activation(
-                    out=xw[n][:, cols], in_=xb[c][:, cols].bitcast(E4M3), func=ACT.Copy, scale=xs[c][:, k : k + 1]
+                    out=xw[n][:, cols], in_=xb[c][:, cols].bitcast(E4M3), func=ACT.Copy, scale=xs[:, c, k : k + 1]
                 )
 
         def turn(n, h, eng):
@@ -151,10 +151,9 @@ def tile_efficientspladecentredscores_d1p_kernel(
             kind, c = chunks[n]
             width = P * tiles_of[n]
             mm = banks.pop((n, vt))
-            sub = tiles_of[n] // 2
             nc.vector.tensor_reduce(
-                out=pooled[kind][:, vt, 64 * c : 64 * (c + 1)].rearrange("p (e d) -> p e d", e=sub),
-                in_=mm[:, :width].rearrange("p (e i d l) -> p e d i l", e=sub, i=2, l=2 * sub),
+                out=pooled[kind][:, vt, 64 * c : 64 * (c + 1)],
+                in_=mm[:, :width].rearrange("p (i d l) -> p d i l", i=tiles_of[n], l=2),
                 axis=AX.XY,
                 op=ALU.max,
             )
@@ -169,41 +168,28 @@ def tile_efficientspladecentredscores_d1p_kernel(
             tp = psum.tile([P, P], F32, name="tpv", tag="tp", bufs=2)
             nc.tensor.transpose(tp[:], vrows_f[:], ident[:])
             nc.scalar.copy(out=vcols[:], in_=tp[:, :24])
-            nc.gpsimd.tensor_scalar(out=nb[:], in0=vcols[:, 0:VT], scalar1=-1.0, scalar2=0.0, op0=ALU.mult, op1=ALU.add)
-            nc.gpsimd.tensor_scalar(out=b1[:], in0=vcols[:, 0:VT], scalar1=1.0, scalar2=1.0, op0=ALU.mult, op1=ALU.add)
+
+        def vector_constants():
+            nc.vector.tensor_scalar(out=nb[:], in0=vcols[:, 0:VT], scalar1=-1.0, scalar2=None, op0=ALU.mult)
+            nc.vector.tensor_scalar(out=b1[:], in0=vcols[:, 0:VT], scalar1=1.0, scalar2=None, op0=ALU.add)
+            for k, count in enumerate((NQ, ND)):
+                nc.vector.tensor_scalar(
+                    out=gneg[:, VT * k : VT * (k + 1)], in0=vcols[:, VT + VT * k : 2 * VT + VT * k], scalar1=-1.0 / count, scalar2=None, op0=ALU.mult
+                )
 
         logs = {
             "q": keep.tile([P, VT, NQ], F32, name="logs_q", align_bytes=64),
             "d": keep.tile([P, VT, ND], F32, name="logs_d", align_bytes=64),
         }
-        sums = {
-            "q": keep.tile([P, VT], F32, name="sums_q", align_bytes=64),
-            "d": keep.tile([P, VT], F32, name="sums_d", align_bytes=64),
-            "d2": keep.tile([P, 1], F32, name="sums_d2", align_bytes=64),
-        }
-        offs = {
-            "q": keep.tile([P, VT], F32, name="off_q", align_bytes=64),
-            "d": keep.tile([P, VT], F32, name="off_d", align_bytes=64),
-        }
+        sums_q = keep.tile([P, VT], F32, name="sums_q", align_bytes=64)
+        sums_d = [keep.tile([P, VT], F32, name="sums_d%d" % k, align_bytes=64) for k in range(2)]
+        last_sum = keep.tile([P, 1], F32, name="last_sum", align_bytes=64)
+        pair_sum = keep.tile([P, 1], F32, name="pair_sum", align_bytes=64)
+        off_q = keep.tile([P, VT], F32, name="off_q", align_bytes=64)
+        off_a = keep.tile([P, VT], F32, name="off_a", align_bytes=64)
+        off_s = keep.tile([P, VT], F32, name="off_s", align_bytes=64)
         off_g = keep.tile([P, VT], F32, name="off_g", align_bytes=64)
         off_v = keep.tile([P, VT], F32, name="off_v", align_bytes=64)
-
-        def negative_gains():
-            for k, count in enumerate((NQ, ND)):
-                cols = slice(VT * k, VT * (k + 1))
-                nc.gpsimd.tensor_scalar(
-                    out=gneg[:, cols], in0=vcols[:, VT + VT * k : 2 * VT + VT * k], scalar1=-1.0 / count, scalar2=0.0, op0=ALU.mult, op1=ALU.add
-                )
-
-        def clip(eng, kind, vt, lo, hi):
-            x = pooled[kind][:, vt, lo:hi]
-            eng.tensor_scalar(out=x, in0=x, scalar1=BIG, scalar2=nb[:, vt : vt + 1], op0=ALU.min, op1=ALU.max)
-
-        def log(kind, vt, lo, hi, acc):
-            nc.scalar.activation(
-                out=logs[kind][:, vt, lo:hi], in_=pooled[kind][:, vt, lo:hi], func=ACT.Ln, bias=b1[:, vt : vt + 1], accum_out=acc
-            )
-
         cg = {
             "q": [keep.tile([P, NQ, 4], BF16, name="cg_q%d" % g, align_bytes=64) for g in range(2)],
             "d": [keep.tile([P, ND, 4], BF16, name="cg_d%d" % g, align_bytes=64) for g in range(2)],
@@ -217,65 +203,42 @@ def tile_efficientspladecentredscores_d1p_kernel(
             "d": keep.tile([P, 2, ND], U8, name="ccs_d", align_bytes=64),
         }
 
-        def shift(vt):
-            col = slice(vt, vt + 1)
-            gain = gneg[:, VT + vt : VT + vt + 1]
-            if vt < 0:
-                nc.gpsimd.tensor_scalar(out=off_g[:, col], in0=sums["d"][:, col], scalar1=gain, scalar2=0.0, op0=ALU.mult, op1=ALU.add)
-            elif vt < 6:
-                nc.scalar.activation(out=offs["d"][:, col], in_=sums["d"][:, col], func=ACT.Copy, scale=gain)
-            elif vt < 7:
-                nc.vector.tensor_scalar(out=off_v[:, col], in0=sums["d"][:, col], scalar1=gain, scalar2=0.0, op0=ALU.mult, op1=ALU.add)
-            else:
-                nc.vector.tensor_scalar(out=off_v[:, col], in0=sums["d"][:, col], scalar1=sums["d2"][:], scalar2=gain, op0=ALU.add, op1=ALU.mult)
+        def clip(eng, kind, vt, lo, hi):
+            x = pooled[kind][:, vt, lo:hi]
+            eng.tensor_scalar(out=x, in0=x, scalar1=BIG, scalar2=nb[:, vt : vt + 1], op0=ALU.min, op1=ALU.max)
 
-        def off(kind, vt):
-            t = offs[kind] if kind == "q" else (off_g if vt < 0 else (offs["d"] if vt < 6 else off_v))
-            return t[:, vt : vt + 1]
-
-        def shift_q(g):
-            cols = slice(4 * g, 4 * g + 4)
-            nc.gpsimd.tensor_tensor(out=offs["q"][:, cols], in0=sums["q"][:, cols], in1=gneg[:, cols], op=ALU.mult)
-
-        def relu_log(kind, vt, lo, hi, acc):
+        def relu(kind, vt, lo, hi):
             x = pooled[kind][:, vt, lo:hi]
             nc.scalar.activation(out=x, in_=x, func=ACT.Relu, bias=vcols[:, vt : vt + 1])
-            nc.scalar.activation(out=logs[kind][:, vt, lo:hi], in_=x, func=ACT.Ln, bias=ones[:], accum_out=acc)
 
-        def centre_g(kind, vt):
-            g, j = vt // 4, vt % 4
-            gain = (8 if kind == "q" else 16) + vt
-            nc.gpsimd.tensor_scalar(
-                out=cg[kind][g][:, :, j],
-                in0=logs[kind][:, vt, :],
-                scalar1=vcols[:, gain : gain + 1],
-                scalar2=off(kind, vt),
-                op0=ALU.mult,
-                op1=ALU.add,
-            )
-
-        def centre_s(kind, vt):
-            g, j = vt // 4, vt % 4
-            gain = (8 if kind == "q" else 16) + vt
+        def ln(kind, vt, lo, hi, acc, clipped):
             nc.scalar.activation(
-                out=cg[kind][g][:, :, j],
-                in_=logs[kind][:, vt, :],
-                func=ACT.Identity,
-                scale=vcols[:, gain : gain + 1],
-                bias=off(kind, vt),
+                out=logs[kind][:, vt, lo:hi],
+                in_=pooled[kind][:, vt, lo:hi],
+                func=ACT.Ln,
+                bias=(b1[:, vt : vt + 1] if clipped else ones[:]),
+                accum_out=acc[:, vt : vt + 1],
             )
 
-        def centre_v(kind, vt):
+        def gain(kind, vt):
+            k = (8 if kind == "q" else 16) + vt
+            return vcols[:, k : k + 1]
+
+        def centre(eng, kind, vt, off):
             g, j = vt // 4, vt % 4
-            gain = (8 if kind == "q" else 16) + vt
-            nc.vector.tensor_scalar(
-                out=cg[kind][g][:, :, j],
-                in0=logs[kind][:, vt, :],
-                scalar1=vcols[:, gain : gain + 1],
-                scalar2=off(kind, vt),
-                op0=ALU.mult,
-                op1=ALU.add,
-            )
+            if eng == "s":
+                nc.scalar.activation(
+                    out=cg[kind][g][:, :, j], in_=logs[kind][:, vt, :], func=ACT.Identity, scale=gain(kind, vt), bias=off[:, vt : vt + 1]
+                )
+            else:
+                (nc.vector if eng == "v" else nc.gpsimd).tensor_scalar(
+                    out=cg[kind][g][:, :, j],
+                    in0=logs[kind][:, vt, :],
+                    scalar1=gain(kind, vt),
+                    scalar2=off[:, vt : vt + 1],
+                    op0=ALU.mult,
+                    op1=ALU.add,
+                )
 
         def quantize_centred(kind, g):
             nc.vector.quantize_mx(
@@ -294,139 +257,172 @@ def tile_efficientspladecentredscores_d1p_kernel(
         turn(0, 0, "v")
         quantize(0)
         permute(0, 1, nc.vector)
-        if -1 < 0:
-            turn(1, 0, "v")
+        if 1 < 0:
+            turn(1, 0, "s")
         widen(2, 0, 16)
 
         order = [(n, vt) for n in range(4) for vt in range(VT)]
-        LEAD = 0
         last = (0, 4, 1, 5, 2, 3, 6, 7)
+        LEAD = 0
         order += [(4, vt) for vt in last[:LEAD]]
         for k, vt in enumerate(last):
             if k + LEAD < VT:
                 order.append((4, last[k + LEAD]))
             order.append((5, vt))
         AHEAD = 2
-
-        late = []
-
-        def finish_shift():
-            if late:
-                if late[0] < 6:
-                    shift(late[0])
-                if late[0] < 4:
-                    centre_g("d", late[0])
-
-        def finish_centre():
-            if late:
-                k = late.pop()
-                if 4 <= k < 6:
-                    centre_s("d", k)
+        GROUP = 2
+        pools = [order[k + GROUP - 1 - m] for k in range(0, len(order) - 2, GROUP) for m in range(GROUP)]
+        pools += order[len(pools):]
+        SPLIT = 128
+        VECTOR = (6, 7)
+        GPS = (0, 1)
+        seen = set()
 
         def query_logs(lo, hi):
             for k in range(lo, hi):
                 if 0 == 2:
-                    relu_log("q", k, 0, NQ, sums["q"][:, k : k + 1])
-                else:
-                    log("q", k, 0, NQ, sums["q"][:, k : k + 1])
+                    relu("q", k, 0, NQ)
+                ln("q", k, 0, NQ, sums_q, 0 != 2)
+            for k in range(lo, hi):
                 if k % 4 == 3:
-                    shift_q(k // 4)
-                    for m in range(k - 3, k + 1):
-                        if m < 0:
-                            centre_g("q", m)
+                    cols = slice(k - 3, k + 1)
+                    nc.vector.tensor_tensor(out=off_q[:, cols], in0=sums_q[:, cols], in1=gneg[:, cols], op=ALU.mult)
 
-        GROUP = 2
-        pools = [order[k + GROUP - 1 - m] for k in range(0, len(order), GROUP) for m in range(GROUP)]
-        seen = set()
+        def query_centres(lo, hi):
+            for m in range(lo, hi):
+                centre("g" if m < 8 else "s", "q", m, off_q)
+
+        def early(lo, hi):
+            for k in range(lo, hi):
+                if k < 0:
+                    clip(nc.gpsimd, "d", k, 0, SPLIT)
+                elif k < 0:
+                    clip(nc.vector, "d", k, 0, SPLIT)
+                else:
+                    relu("d", k, 0, SPLIT)
+            for k in range(lo, hi):
+                ln("d", k, 0, SPLIT, sums_d[0], k < 0)
+            for k in range(lo, hi):
+                if k not in VECTOR + GPS:
+                    nc.scalar.activation(out=off_a[:, k : k + 1], in_=sums_d[0][:, k : k + 1], func=ACT.Copy, scale=gneg[:, VT + k : VT + k + 1])
+
+        def offset(k):
+            col = slice(k, k + 1)
+            dcol = gneg[:, VT + k : VT + k + 1]
+            if k in VECTOR or k in GPS:
+                eng, dst = (nc.vector, off_v) if k in VECTOR else (nc.gpsimd, off_g)
+                if SPLIT == 0:
+                    eng.tensor_scalar(out=dst[:, col], in0=sums_d[1][:, col], scalar1=dcol, scalar2=0.0, op0=ALU.mult, op1=ALU.add)
+                else:
+                    eng.tensor_scalar(
+                        out=dst[:, col], in0=sums_d[1][:, col], scalar1=sums_d[0][:, col], scalar2=dcol, op0=ALU.add, op1=ALU.mult
+                    )
+            elif SPLIT == 0:
+                nc.scalar.activation(out=off_s[:, col], in_=sums_d[1][:, col], func=ACT.Copy, scale=dcol)
+            else:
+                nc.scalar.activation(
+                    out=off_s[:, col], in_=sums_d[1][:, col], func=ACT.Identity, scale=dcol, bias=off_a[:, col]
+                )
+
+        def final_centre(k):
+            if k in VECTOR:
+                centre("v", "d", k, off_v)
+            elif k in GPS:
+                centre("g", "d", k, off_g)
+            else:
+                centre("s", "d", k, off_s)
+
+        late = []
         for i in range(AHEAD):
             scores(*order[i])
         for i, (n, vt) in enumerate(pools):
             if i + AHEAD < len(order):
                 scores(*order[i + AHEAD])
+            if i == len(pools) - 1:
+                relu("d", 7, SPLIT, 192)
+                ln("d", 7, SPLIT, 192, sums_d[1], False)
             pool(n, vt)
             seen.add((n, vt))
             if i == 4:
                 permute(1, 0, nc.vector)
-            if i == 3:
+            if i == 8:
                 permute(1, 1, nc.vector)
-            if i == -1:
-                turn(1, 0, "v")
-            if i == 0:
+            if i == 1:
+                turn(1, 0, "s")
+            if i == 2:
                 quantize(1)
-            if i == 6:
+            if i == 4:
                 nc.vector.tensor_copy(out=vrows_f[:], in_=vrows[:])
-            if i == 3:
+            if i == 5:
                 turn(2, 0, "s")
                 turn(2, 1, "s")
-                widen(3, 0, 16)
-            if i == 7:
+            if i == 5:
                 vector_columns()
-            if 8 <= i < 16:
-                if 0 == 0:
-                    clip(nc.gpsimd, "q", vt, 0, NQ)
-                elif 0 == 1:
-                    clip(nc.vector, "q", vt, 0, NQ)
-                if i == 15:
-                    negative_gains()
-            if i == 11:
+                vector_constants()
+                widen(3, 0, 16)
+            if 0 == 1 and 10 <= i < 18:
+                clip(nc.vector, "q", pools[i - 2][1], 0, NQ)
+            if 0 == 0 and 8 <= i < 16:
+                clip(nc.gpsimd, "q", vt, 0, NQ)
+            if i == 7:
                 quantize(2)
-            if i == 13:
+            if i == 10:
                 turn(3, 0, "s")
                 turn(3, 1, "s")
                 widen(4, 0, 16)
-            if i == 16:
-                query_logs(0, 0)
+            if i == 18:
+                query_logs(0, 4)
+                query_centres(0, 4)
             if i == 17:
                 quantize(3)
-            if i == 20:
+            if i == 18:
                 turn(4, 0, "s")
                 turn(4, 1, "s")
+                query_logs(4, 4)
+                query_centres(4, 4)
                 widen(5, 0, 16)
-                query_logs(0, 0)
-            if i == 29:
+            if i == 23:
                 quantize(4)
             if i == 27:
                 turn(5, 0, "s")
                 turn(5, 1, "s")
-                query_logs(0, 8)
-                for m in range(0, 8):
-                    centre_s("q", m)
+            if i == 27 + 1:
+                query_logs(4, 8)
+                query_centres(4, 8)
             if i == 28:
                 quantize(5)
+            if i == 32 and SPLIT > 0:
+                early(0, VT)
             if n >= 4 and vt < 7 and (4, vt) in seen and (5, vt) in seen:
-                x = pooled["d"][:, vt, :]
-                if vt < 3:
-                    clip(nc.gpsimd, "d", vt, 0, ND)
-                elif vt < 4:
-                    clip(nc.vector, "d", vt, 0, ND)
-                finish_shift()
-                if vt >= 4:
-                    nc.scalar.activation(out=x, in_=x, func=ACT.Relu, bias=vcols[:, vt : vt + 1])
-                finish_centre()
-                nc.scalar.activation(
-                    out=logs["d"][:, vt, :],
-                    in_=x,
-                    func=ACT.Ln,
-                    bias=(b1[:, vt : vt + 1] if vt < 4 else ones[:]),
-                    accum_out=sums["d"][:, vt : vt + 1],
-                )
-                late.append(vt)
-            if i == 43:
+                if vt < 0:
+                    clip(nc.gpsimd, "d", vt, SPLIT, ND)
+                elif vt < 0:
+                    clip(nc.vector, "d", vt, SPLIT, ND)
+                for k in late:
+                    offset(k)
+                if vt >= 0:
+                    relu("d", vt, SPLIT, ND)
+                for k in late:
+                    final_centre(k)
+                ln("d", vt, SPLIT, ND, sums_d[1], vt < 0)
+                late = [vt]
+            if i == 44:
                 quantize_centred("q", 0)
                 quantize_centred("q", 1)
-        x = pooled["d"][:, 7, 0:192]
-        nc.scalar.activation(out=x, in_=x, func=ACT.Relu, bias=vcols[:, 7:8])
-        finish_shift()
-        nc.scalar.activation(out=logs["d"][:, 7, 0:192], in_=x, func=ACT.Ln, bias=ones[:], accum_out=sums["d2"][:])
-        finish_centre()
-        x = pooled["d"][:, 7, 192:256]
-        nc.scalar.activation(out=x, in_=x, func=ACT.Relu, bias=vcols[:, 7:8])
-        nc.scalar.activation(out=logs["d"][:, 7, 192:256], in_=x, func=ACT.Ln, bias=ones[:], accum_out=sums["d"][:, 7:8])
-        shift(6)
-        centre_v("d", 6)
-        shift(7)
+        relu("d", 7, 192, ND)
+        nc.scalar.activation(
+            out=logs["d"][:, 7, 192:ND], in_=pooled["d"][:, 7, 192:ND], func=ACT.Ln, bias=ones[:], accum_out=last_sum[:]
+        )
+        for k in late:
+            offset(k)
+            final_centre(k)
+        if SPLIT > 0:
+            nc.vector.tensor_tensor(out=pair_sum[:], in0=sums_d[1][:, 7:8], in1=sums_d[0][:, 7:8], op=ALU.add)
         quantize_centred("d", 0)
-        centre_v("d", 7)
+        nc.vector.tensor_scalar(
+            out=off_v[:, 7:8], in0=last_sum[:], scalar1=(pair_sum[:] if SPLIT > 0 else sums_d[1][:, 7:8]), scalar2=gneg[:, 15:16], op0=ALU.add, op1=ALU.mult
+        )
+        centre("v", "d", 7, off_v)
         outs = [psum.tile([P, 512], F32, name="mm", tag="mm", bufs=6) for h in range(2)]
         for g in range(2):
             if g == 1:

@@ -29,7 +29,7 @@ def tile_efficientspladecentredscores_d1p_kernel(
         keep = ctx.enter_context(tc.tile_pool(name="keep", bufs=1))
         psum = ctx.enter_context(tc.psum_pool(name="psum", bufs=1))
 
-        xq_rows = xq.rearrange("n l d -> (n l) d").rearrange("(c p i) d -> c p (i d)", c=2, i=2)
+        xq_rows = xq.rearrange("n l d -> (n l) d").rearrange("(c p i) d -> p c (i d)", c=2, i=2)
         xd_rows = xd_bytes.rearrange("n l d -> (n l) d").rearrange("(c p i) d -> c p (i d)", c=4, i=4)
         xs_rows = xd_scale.rearrange("n l j -> (n l) j").rearrange("(c p i) j -> p c (i j)", c=4, i=4)
 
@@ -38,14 +38,14 @@ def tile_efficientspladecentredscores_d1p_kernel(
         ones = keep.tile([P, 1], F32, name="ones", align_bytes=64)
         nc.vector.memset(ones[:], 1.0)
         ws_raw = [keep.tile([P, V], U8, name="ws_raw%d" % s, align_bytes=64) for s in range(2)]
-        vrows = keep.tile([P, P], BF16, name="vrows", align_bytes=64)
+        vrows = keep.tile([P, 2 * P], BF16, name="vrows", align_bytes=64)
         ident = keep.tile([P, P], F32, name="ident", align_bytes=64)
         for s in range(2):
             nc.vector.memset(ws_raw[s][:].bitcast(I32), 0)
         nc.vector.memset(vrows[:], 0.0)
         make_identity(nc, ident[:])
 
-        xw_q = [keep.tile([P, 2 * D], BF16, name="xw_q%d" % c, align_bytes=64) for c in range(2)]
+        xw_q = keep.tile([P, 2, 2 * D], BF16, name="xw_q", align_bytes=64)
         xb = [keep.tile([P, 4 * D], U8, name="xb%d" % c, align_bytes=64) for c in range(4)]
         xs = keep.tile([P, 4, 16], F32, name="xs", align_bytes=64)
         ww_raw = [keep.tile([P, 2 * V], U8, name="ww_raw%d" % s, align_bytes=64) for s in range(2)]
@@ -62,27 +62,23 @@ def tile_efficientspladecentredscores_d1p_kernel(
                     in_=scales[s][0, 4 * q : 4 * q + 4, :].bitcast(I32),
                 )
 
-        load_scales(0, nc.scalar)
-        nc.sync.dma_start(out=xw_q[0][:], in_=xq_rows[0])
+        nc.sync.dma_start(out=xw_q[:], in_=xq_rows)
+        load_scales(0, nc.sync)
         load_words(0)
         warm = keep.tile([P, 1], F32, name="warm", align_bytes=64)
         nc.scalar.activation(out=warm[:], in_=ones[:], func=ACT.Ln)
         nc.sync.dma_start(out=xb[0][:], in_=xd_rows[0])
-        nc.sync.dma_start(out=xs[:, 0, :], in_=xs_rows[:, 0, :])
-        nc.sync.dma_start(out=xw_q[1][:], in_=xq_rows[1])
+        nc.sync.dma_start(out=xs[:], in_=xs_rows)
         nc.sync.dma_start(out=xb[1][:], in_=xd_rows[1])
-        nc.sync.dma_start(out=xs[:, 1:, :], in_=xs_rows[:, 1:, :])
+        for i, vec in enumerate((b, gq, gd)):
+            nc.sync.dma_start(
+                out=vrows[4 * i : 4 * i + 4, :].rearrange("j (h r) -> j h r", r=8),
+                in_=vec.rearrange("(h j r) -> j h r", j=4, r=8),
+            )
         load_words(1)
         load_scales(1, nc.sync)
         nc.sync.dma_start(out=xb[2][:], in_=xd_rows[2])
         nc.sync.dma_start(out=xb[3][:], in_=xd_rows[3])
-        for i, vec in enumerate((b, gq, gd)):
-            halves = vec.rearrange("(g q j r) -> g j q r", g=2, q=16, j=4)
-            for g in range(2):
-                r0 = 8 * i + 4 * g
-                nc.sync.dma_start(
-                    out=vrows[r0 : r0 + 4, :].rearrange("j (q r) -> j q r", q=16), in_=halves[g]
-                )
         ww = [keep.tile([P, 2 * V], U8, name="ww%d" % s, align_bytes=64) for s in range(2)]
         ws = [keep.tile([P, V], U8, name="ws%d" % s, align_bytes=64) for s in range(2)]
 
@@ -96,7 +92,7 @@ def tile_efficientspladecentredscores_d1p_kernel(
 
         chunks = [("q", 0), ("q", 1), ("d", 0), ("d", 1), ("d", 2), ("d", 3)]
         tiles_of = [2, 2, 4, 4, 4, 4]
-        xw = list(xw_q) + [keep.tile([P, 4 * D], BF16, name="xw_d%d" % c, align_bytes=64) for c in range(4)]
+        xw = [xw_q[:, 0, :], xw_q[:, 1, :]] + [keep.tile([P, 4 * D], BF16, name="xw_d%d" % c, align_bytes=64) for c in range(4)]
         xg = [keep.tile([P, 4 * P * tiles_of[n]], BF16, name="xg%d" % n, align_bytes=64) for n in range(6)]
         xc = [keep.tile([P, P * tiles_of[n]], U32, name="xc%d" % n, align_bytes=64) for n in range(6)]
         xcs = [keep.tile([P, P * tiles_of[n]], U8, name="xcs%d" % n, align_bytes=64) for n in range(6)]
@@ -111,13 +107,25 @@ def tile_efficientspladecentredscores_d1p_kernel(
 
         def turn(n, h, eng):
             tp = psum.tile([P, 2, 2, P], F32, name="tp", tag="tp", bufs=2)
-            pairs = xw[n][:].bitcast(F32)
+            pairs = (xw[n] if n < 2 else xw[n][:]).bitcast(F32)
             for i in range(2):
                 for u in range(2):
                     c0 = 256 * (2 * h + i)
                     nc.tensor.transpose(tp[:, i, u, :], pairs[:, c0 + u : c0 + 256 : 2], ident[:])
             dst = xg[n][:].bitcast(F32)[:, 512 * h : 512 * (h + 1)].rearrange("p (i r u) -> p i r u", i=2, u=2)
             src = tp[:].rearrange("p i u r -> p i r u")
+            if eng == "v":
+                nc.vector.tensor_copy(out=dst, in_=src)
+            else:
+                nc.scalar.copy(out=dst, in_=src)
+
+        def turn_tile(n, i, eng):
+            tp = psum.tile([P, 2, P], F32, name="tpt", tag="tp", bufs=2)
+            pairs = (xw[n] if n < 2 else xw[n][:]).bitcast(F32)
+            for u in range(2):
+                nc.tensor.transpose(tp[:, u, :], pairs[:, 256 * i + u : 256 * (i + 1) : 2], ident[:])
+            dst = xg[n][:].bitcast(F32)[:, 256 * i : 256 * (i + 1)].rearrange("p (r u) -> p r u", u=2)
+            src = tp[:].rearrange("p u r -> p r u")
             if eng == "v":
                 nc.vector.tensor_copy(out=dst, in_=src)
             else:
@@ -162,19 +170,29 @@ def tile_efficientspladecentredscores_d1p_kernel(
         nb = keep.tile([P, VT], F32, name="nb", align_bytes=64)
         b1 = keep.tile([P, VT], F32, name="b1", align_bytes=64)
         gneg = keep.tile([P, 2 * VT], F32, name="gneg", align_bytes=64)
-        vrows_f = keep.tile([P, P], F32, name="vrows_f", align_bytes=64)
+        vrows_f = keep.tile([P, 2 * P], F32, name="vrows_f", align_bytes=64)
 
         def vector_columns():
-            tp = psum.tile([P, P], F32, name="tpv", tag="tp", bufs=2)
-            nc.tensor.transpose(tp[:], vrows_f[:], ident[:])
-            nc.scalar.copy(out=vcols[:], in_=tp[:, :24])
+            tp = psum.tile([P, 2, P], F32, name="tpv", tag="tp", bufs=2)
+            for g in range(2):
+                nc.tensor.transpose(tp[:, g, :], vrows_f[:, P * g : P * (g + 1)], ident[:])
+            nc.scalar.copy(
+                out=vcols[:].rearrange("p (v g j) -> p v g j", v=3, g=2),
+                in_=tp[:, :, :12].rearrange("p g (v j) -> p v g j", v=3),
+            )
 
         def vector_constants():
-            nc.vector.tensor_scalar(out=nb[:], in0=vcols[:, 0:VT], scalar1=-1.0, scalar2=None, op0=ALU.mult)
-            nc.vector.tensor_scalar(out=b1[:], in0=vcols[:, 0:VT], scalar1=1.0, scalar2=None, op0=ALU.add)
+            eng = nc.vector
+            eng.tensor_scalar(out=nb[:], in0=vcols[:, 0:VT], scalar1=-1.0, scalar2=0.0, op0=ALU.mult, op1=ALU.add)
+            eng.tensor_scalar(out=b1[:], in0=vcols[:, 0:VT], scalar1=1.0, scalar2=1.0, op0=ALU.mult, op1=ALU.add)
             for k, count in enumerate((NQ, ND)):
-                nc.vector.tensor_scalar(
-                    out=gneg[:, VT * k : VT * (k + 1)], in0=vcols[:, VT + VT * k : 2 * VT + VT * k], scalar1=-1.0 / count, scalar2=None, op0=ALU.mult
+                eng.tensor_scalar(
+                    out=gneg[:, VT * k : VT * (k + 1)],
+                    in0=vcols[:, VT + VT * k : 2 * VT + VT * k],
+                    scalar1=-1.0 / count,
+                    scalar2=0.0,
+                    op0=ALU.mult,
+                    op1=ALU.add,
                 )
 
         logs = {
@@ -183,15 +201,13 @@ def tile_efficientspladecentredscores_d1p_kernel(
         }
         sums_q = keep.tile([P, VT], F32, name="sums_q", align_bytes=64)
         sums_d = [keep.tile([P, VT], F32, name="sums_d%d" % k, align_bytes=64) for k in range(2)]
-        last_sum = keep.tile([P, 1], F32, name="last_sum", align_bytes=64)
-        pair_sum = keep.tile([P, 1], F32, name="pair_sum", align_bytes=64)
         off_q = keep.tile([P, VT], F32, name="off_q", align_bytes=64)
         off_a = keep.tile([P, VT], F32, name="off_a", align_bytes=64)
         off_s = keep.tile([P, VT], F32, name="off_s", align_bytes=64)
         off_g = keep.tile([P, VT], F32, name="off_g", align_bytes=64)
         off_v = keep.tile([P, VT], F32, name="off_v", align_bytes=64)
         cg = {
-            "q": [keep.tile([P, NQ, 4], BF16, name="cg_q%d" % g, align_bytes=64) for g in range(2)],
+            "q": keep.tile([P, 2, NQ, 4], BF16, name="cg_q", align_bytes=64),
             "d": [keep.tile([P, ND, 4], BF16, name="cg_d%d" % g, align_bytes=64) for g in range(2)],
         }
         cc = {
@@ -224,15 +240,25 @@ def tile_efficientspladecentredscores_d1p_kernel(
             k = (8 if kind == "q" else 16) + vt
             return vcols[:, k : k + 1]
 
+        cu = keep.tile([P, 4, ND], BF16, name="cu", align_bytes=64)
+
+        def slot(kind, g, j):
+            if kind == "q":
+                return cg["q"][:, g, :, j]
+            return cu[:, j, :] if g == 1 and 1 else cg["d"][g][:, :, j]
+
+        def interleave(lo, hi):
+            nc.vector.tensor_copy(out=cg["d"][1][:, lo:hi, :], in_=cu[:, :, lo:hi].rearrange("p j d -> p d j"))
+
         def centre(eng, kind, vt, off):
             g, j = vt // 4, vt % 4
             if eng == "s":
                 nc.scalar.activation(
-                    out=cg[kind][g][:, :, j], in_=logs[kind][:, vt, :], func=ACT.Identity, scale=gain(kind, vt), bias=off[:, vt : vt + 1]
+                    out=slot(kind, g, j), in_=logs[kind][:, vt, :], func=ACT.Identity, scale=gain(kind, vt), bias=off[:, vt : vt + 1]
                 )
             else:
                 (nc.vector if eng == "v" else nc.gpsimd).tensor_scalar(
-                    out=cg[kind][g][:, :, j],
+                    out=slot(kind, g, j),
                     in0=logs[kind][:, vt, :],
                     scalar1=gain(kind, vt),
                     scalar2=off[:, vt : vt + 1],
@@ -240,11 +266,18 @@ def tile_efficientspladecentredscores_d1p_kernel(
                     op1=ALU.add,
                 )
 
-        def quantize_centred(kind, g):
+        def quantize_queries():
             nc.vector.quantize_mx(
-                out=cc[kind][:, g, :].bitcast(E4M3X4),
-                scales=ccs[kind][:, g, :],
-                in_=cg[kind][g][:].rearrange("p d j -> p (d j)"),
+                out=cc["q"][:].rearrange("p g n -> p (g n)").bitcast(E4M3X4),
+                scales=ccs["q"][:].rearrange("p g n -> p (g n)"),
+                in_=cg["q"][:].rearrange("p g n j -> p (g n j)"),
+            )
+
+        def quantize_docs(g, lo, hi):
+            nc.vector.quantize_mx(
+                out=cc["d"][:, g, lo:hi].bitcast(E4M3X4),
+                scales=ccs["d"][:, g, lo:hi],
+                in_=cg["d"][g][:, lo:hi, :].rearrange("p d j -> p (d j)"),
             )
 
         idle = keep.tile([P, 512], BF16, name="idle", align_bytes=64)
@@ -253,40 +286,42 @@ def tile_efficientspladecentredscores_d1p_kernel(
         for k in range(4):
             nc.tensor.matmul(wake[:], lhsT=idle[:, :P], rhs=idle[:], start=True, stop=True)
 
+        turn_tile(0, 0, "v")
+        turn_tile(0, 1, "s")
         permute(0, 0, nc.vector)
-        turn(0, 0, "v")
         quantize(0)
         permute(0, 1, nc.vector)
-        if 1 < 0:
-            turn(1, 0, "s")
+        if -1 < 0:
+            turn_tile(1, 0, "v")
+            turn_tile(1, 1, "v")
         widen(2, 0, 16)
 
         order = [(n, vt) for n in range(4) for vt in range(VT)]
-        last = (0, 4, 1, 5, 2, 3, 6, 7)
-        LEAD = 0
+        last = (0, 1, 2, 3, 4, 5, 6, 7)
+        LEAD = 2
         order += [(4, vt) for vt in last[:LEAD]]
         for k, vt in enumerate(last):
             if k + LEAD < VT:
                 order.append((4, last[k + LEAD]))
             order.append((5, vt))
-        AHEAD = 2
+        AHEAD = 3
         GROUP = 2
-        pools = [order[k + GROUP - 1 - m] for k in range(0, len(order) - 2, GROUP) for m in range(GROUP)]
+        pools = [order[k + GROUP - 1 - m] for k in range(0, len(order) - GROUP, GROUP) for m in range(GROUP)]
         pools += order[len(pools):]
         SPLIT = 128
         VECTOR = (6, 7)
-        GPS = (0, 1)
+        GPS = (0, 1, 4)
         seen = set()
 
         def query_logs(lo, hi):
             for k in range(lo, hi):
-                if 0 == 2:
+                if 1 == 2:
                     relu("q", k, 0, NQ)
-                ln("q", k, 0, NQ, sums_q, 0 != 2)
+                ln("q", k, 0, NQ, sums_q, 1 != 2)
             for k in range(lo, hi):
                 if k % 4 == 3:
                     cols = slice(k - 3, k + 1)
-                    nc.vector.tensor_tensor(out=off_q[:, cols], in0=sums_q[:, cols], in1=gneg[:, cols], op=ALU.mult)
+                    nc.gpsimd.tensor_tensor(out=off_q[:, cols], in0=sums_q[:, cols], in1=gneg[:, cols], op=ALU.mult)
 
         def query_centres(lo, hi):
             for m in range(lo, hi):
@@ -303,13 +338,13 @@ def tile_efficientspladecentredscores_d1p_kernel(
             for k in range(lo, hi):
                 ln("d", k, 0, SPLIT, sums_d[0], k < 0)
             for k in range(lo, hi):
-                if k not in VECTOR + GPS:
+                if k not in VECTOR + GPS and not 0:
                     nc.scalar.activation(out=off_a[:, k : k + 1], in_=sums_d[0][:, k : k + 1], func=ACT.Copy, scale=gneg[:, VT + k : VT + k + 1])
 
         def offset(k):
             col = slice(k, k + 1)
             dcol = gneg[:, VT + k : VT + k + 1]
-            if k in VECTOR or k in GPS:
+            if k in VECTOR or k in GPS or 0:
                 eng, dst = (nc.vector, off_v) if k in VECTOR else (nc.gpsimd, off_g)
                 if SPLIT == 0:
                     eng.tensor_scalar(out=dst[:, col], in0=sums_d[1][:, col], scalar1=dcol, scalar2=0.0, op0=ALU.mult, op1=ALU.add)
@@ -330,7 +365,7 @@ def tile_efficientspladecentredscores_d1p_kernel(
             elif k in GPS:
                 centre("g", "d", k, off_g)
             else:
-                centre("s", "d", k, off_s)
+                centre("s", "d", k, off_g if 0 else off_s)
 
         late = []
         for i in range(AHEAD):
@@ -338,97 +373,111 @@ def tile_efficientspladecentredscores_d1p_kernel(
         for i, (n, vt) in enumerate(pools):
             if i + AHEAD < len(order):
                 scores(*order[i + AHEAD])
-            if i == len(pools) - 1:
-                relu("d", 7, SPLIT, 192)
-                ln("d", 7, SPLIT, 192, sums_d[1], False)
             pool(n, vt)
             seen.add((n, vt))
-            if i == 4:
-                permute(1, 0, nc.vector)
-            if i == 8:
-                permute(1, 1, nc.vector)
-            if i == 1:
-                turn(1, 0, "s")
+            if i == 5:
+                permute(1, 0, nc.gpsimd)
+            if i == 9:
+                permute(1, 1, nc.gpsimd)
+            if i == -1:
+                turn_tile(1, 0, "v")
+                turn_tile(1, 1, "v")
+                widen(2, 16, 16)
             if i == 2:
                 quantize(1)
-            if i == 4:
+            if i == 3:
                 nc.vector.tensor_copy(out=vrows_f[:], in_=vrows[:])
-            if i == 5:
+            if i == 2:
                 turn(2, 0, "s")
                 turn(2, 1, "s")
-            if i == 5:
+            if i == 4:
                 vector_columns()
-                vector_constants()
+                if "vector" == "gpsimd":
+                    vector_constants()
                 widen(3, 0, 16)
-            if 0 == 1 and 10 <= i < 18:
+            if 1 == 1 and 10 <= i < 18:
                 clip(nc.vector, "q", pools[i - 2][1], 0, NQ)
-            if 0 == 0 and 8 <= i < 16:
-                clip(nc.gpsimd, "q", vt, 0, NQ)
-            if i == 7:
+            if 1 == 0 and i == max(16, 4):
+                for k in range(VT):
+                    clip(nc.gpsimd, "q", pools[8 + k][1], 0, NQ)
+            if i == 7 and "vector" == "vector":
+                vector_constants()
+            if i == 11:
                 quantize(2)
-            if i == 10:
+            if i == 12:
                 turn(3, 0, "s")
                 turn(3, 1, "s")
                 widen(4, 0, 16)
             if i == 18:
                 query_logs(0, 4)
                 query_centres(0, 4)
-            if i == 17:
+            if i == 15:
                 quantize(3)
-            if i == 18:
+            if i == 20:
                 turn(4, 0, "s")
                 turn(4, 1, "s")
                 query_logs(4, 4)
                 query_centres(4, 4)
                 widen(5, 0, 16)
-            if i == 23:
+            if i == 24:
                 quantize(4)
-            if i == 27:
+            if i == 26:
                 turn(5, 0, "s")
                 turn(5, 1, "s")
-            if i == 27 + 1:
+            if i == 26 + 1:
                 query_logs(4, 8)
                 query_centres(4, 8)
-            if i == 28:
+            if i == 30:
                 quantize(5)
             if i == 32 and SPLIT > 0:
                 early(0, VT)
             if n >= 4 and vt < 7 and (4, vt) in seen and (5, vt) in seen:
+                if 0 == 1:
+                    for k in late:
+                        offset(k)
                 if vt < 0:
                     clip(nc.gpsimd, "d", vt, SPLIT, ND)
                 elif vt < 0:
                     clip(nc.vector, "d", vt, SPLIT, ND)
-                for k in late:
-                    offset(k)
+                if 0 == 0:
+                    for k in late:
+                        offset(k)
                 if vt >= 0:
                     relu("d", vt, SPLIT, ND)
                 for k in late:
                     final_centre(k)
                 ln("d", vt, SPLIT, ND, sums_d[1], vt < 0)
                 late = [vt]
-            if i == 44:
-                quantize_centred("q", 0)
-                quantize_centred("q", 1)
-        relu("d", 7, 192, ND)
-        nc.scalar.activation(
-            out=logs["d"][:, 7, 192:ND], in_=pooled["d"][:, 7, 192:ND], func=ACT.Ln, bias=ones[:], accum_out=last_sum[:]
-        )
+            if i == 41:
+                quantize_queries()
+            if i == 47:
+                quantize_docs(0, 0, ND)
+        if 1:
+            for k in late:
+                if k not in VECTOR:
+                    offset(k)
+                    final_centre(k)
+            late = [k for k in late if k in VECTOR]
+        relu("d", 7, SPLIT, ND)
+        ln("d", 7, SPLIT, ND, sums_d[1], False)
+        if 47 == 48:
+            quantize_docs(0, 0, ND)
         for k in late:
             offset(k)
             final_centre(k)
-        if SPLIT > 0:
-            nc.vector.tensor_tensor(out=pair_sum[:], in0=sums_d[1][:, 7:8], in1=sums_d[0][:, 7:8], op=ALU.add)
-        quantize_centred("d", 0)
-        nc.vector.tensor_scalar(
-            out=off_v[:, 7:8], in0=last_sum[:], scalar1=(pair_sum[:] if SPLIT > 0 else sums_d[1][:, 7:8]), scalar2=gneg[:, 15:16], op0=ALU.add, op1=ALU.mult
-        )
-        centre("v", "d", 7, off_v)
+        offset(7)
+        final_centre(7)
+        if 47 == 49:
+            quantize_docs(0, 0, ND)
         outs = [psum.tile([P, 512], F32, name="mm", tag="mm", bufs=6) for h in range(2)]
+        if 1:
+            for h in range(2):
+                interleave(P * h, P * (h + 1))
         for g in range(2):
-            if g == 1:
-                quantize_centred("d", 1)
             for h in range(2):
                 cols = slice(P * h, P * (h + 1))
+                if g == 1:
+                    quantize_docs(1, P * h, P * (h + 1))
                 nc.tensor.matmul_mx(
                     out=outs[h][:, :P],
                     lhsT=cc["q"][:, g, :].bitcast(E4M3X4),
@@ -439,7 +488,7 @@ def tile_efficientspladecentredscores_d1p_kernel(
                     stop=(g == 1),
                 )
         res = [keep.tile([P, P], F32, name="res%d" % h, align_bytes=64) for h in range(2)]
-        nc.vector.tensor_copy(out=res[0][:], in_=outs[0][:, :P])
-        nc.sync.dma_start(out=out[:, :P], in_=res[0][:])
-        nc.scalar.copy(out=res[1][:], in_=outs[1][:, :P])
-        nc.scalar.dma_start(out=out[:, P:], in_=res[1][:])
+        nc.scalar.copy(out=res[0][:], in_=outs[0][:, :P])
+        nc.scalar.dma_start(out=out[:, :P], in_=res[0][:])
+        nc.vector.tensor_copy(out=res[1][:], in_=outs[1][:, :P])
+        nc.sync.dma_start(out=out[:, P:], in_=res[1][:])

import concourse.mybir as mybir
from concourse.masks import make_identity
from contextlib import ExitStack

F32 = mybir.dt.float32
BF16 = mybir.dt.bfloat16
I32 = mybir.dt.int32
U32 = mybir.dt.uint32
U8 = mybir.dt.uint8
E4M3 = mybir.dt.float8_e4m3fn
E4M3X4 = mybir.dt.float8_e4m3fn_x4
E2M1X4 = mybir.dt.float4_e2m1fn_x4
ACT = mybir.ActivationFunctionType
ALU = mybir.AluOpType
AX = mybir.AxisListType

P = 128
NQ, LQ, ND, LD, D, V = 128, 4, 256, 8, 512, 1024
VT = V // P
BIG = 3.0e38
FLOPS = 2 * D * V * (NQ * LQ + ND * LD) + 2 * V * NQ * ND


def tile_efficientspladecentredscores_d1p_kernel(
    tc, xq, xd_bytes, xd_scale, wq_words, wq_scales, wd_words, wd_scales, b, gq, gd, out
):
    nc = tc.nc
    with ExitStack() as ctx:
        keep = ctx.enter_context(tc.tile_pool(name="keep", bufs=1))
        psum = ctx.enter_context(tc.psum_pool(name="psum", bufs=1))

        xq_rows = xq.rearrange("n l d -> (n l) d").rearrange("(c p i) d -> p c (i d)", c=2, i=2)
        xd_rows = xd_bytes.rearrange("n l d -> (n l) d").rearrange("(c p i) d -> c p (i d)", c=4, i=4)
        xs_rows = xd_scale.rearrange("n l j -> (n l) j").rearrange("(c p i) j -> p c (i j)", c=4, i=4)

        ctx.enter_context(tc.manual_schedule())

        ones = keep.tile([P, 1], F32, name="ones", align_bytes=64)
        nc.vector.memset(ones[:], 1.0)
        ws_raw = [keep.tile([P, V], U8, name="ws_raw%d" % s, align_bytes=64) for s in range(2)]
        vrows = keep.tile([P, 2 * P], BF16, name="vrows", align_bytes=64)
        ident = keep.tile([P, P], F32, name="ident", align_bytes=64)
        for s in range(2):
            nc.vector.memset(ws_raw[s][:].bitcast(I32), 0)
        nc.vector.memset(vrows[:], 0.0)
        make_identity(nc, ident[:])

        xw_q = keep.tile([P, 2, 2 * D], BF16, name="xw_q", align_bytes=64)
        xb = [keep.tile([P, 4 * D], U8, name="xb%d" % c, align_bytes=64) for c in range(4)]
        xs = keep.tile([P, 4, 16], F32, name="xs", align_bytes=64)
        ww_raw = [keep.tile([P, 2 * V], U8, name="ww_raw%d" % s, align_bytes=64) for s in range(2)]
        words = (wq_words, wd_words)
        scales = (wq_scales, wd_scales)

        def load_words(s):
            nc.sync.dma_start(out=ww_raw[s][:].bitcast(I32), in_=words[s][0].bitcast(I32))

        def load_scales(s, eng):
            for q in range(4):
                eng.dma_start(
                    out=ws_raw[s][32 * q : 32 * q + 4, :].bitcast(I32),
                    in_=scales[s][0, 4 * q : 4 * q + 4, :].bitcast(I32),
                )

        nc.sync.dma_start(out=xw_q[:], in_=xq_rows)
        load_scales(0, nc.sync)
        load_words(0)
        warm = keep.tile([P, 1], F32, name="warm", align_bytes=64)
        nc.scalar.activation(out=warm[:], in_=ones[:], func=ACT.Ln)
        nc.sync.dma_start(out=xb[0][:], in_=xd_rows[0])
        nc.sync.dma_start(out=xs[:], in_=xs_rows)
        nc.sync.dma_start(out=xb[1][:], in_=xd_rows[1])
        for i, vec in enumerate((b, gq, gd)):
            nc.sync.dma_start(
                out=vrows[4 * i : 4 * i + 4, :].rearrange("j (h r) -> j h r", r=8),
                in_=vec.rearrange("(h j r) -> j h r", j=4, r=8),
            )
        load_words(1)
        load_scales(1, nc.sync)
        nc.sync.dma_start(out=xb[2][:], in_=xd_rows[2])
        nc.sync.dma_start(out=xb[3][:], in_=xd_rows[3])
        ww = [keep.tile([P, 2 * V], U8, name="ww%d" % s, align_bytes=64) for s in range(2)]
        ws = [keep.tile([P, V], U8, name="ws%d" % s, align_bytes=64) for s in range(2)]

        def permute(s, g, eng):
            for dst, src, n in ((ww[s], ww_raw[s], 4), (ws[s], ws_raw[s], 2)):
                cols = slice(64 * n * g, 64 * n * (g + 1))
                eng.tensor_copy(
                    out=dst[:].bitcast(I32)[:, cols].rearrange("p (j q s) -> p j q s", j=4, q=16),
                    in_=src[:].bitcast(I32)[:, cols].rearrange("p (q j s) -> p j q s", j=4, q=16),
                )

        chunks = [("q", 0), ("q", 1), ("d", 0), ("d", 1), ("d", 2), ("d", 3)]
        tiles_of = [2, 2, 4, 4, 4, 4]
        xw = [xw_q[:, 0, :], xw_q[:, 1, :]] + [keep.tile([P, 4 * D], BF16, name="xw_d%d" % c, align_bytes=64) for c in range(4)]
        xg = [keep.tile([P, 4 * P * tiles_of[n]], BF16, name="xg%d" % n, align_bytes=64) for n in range(6)]
        xc = [keep.tile([P, P * tiles_of[n]], U32, name="xc%d" % n, align_bytes=64) for n in range(6)]
        xcs = [keep.tile([P, P * tiles_of[n]], U8, name="xcs%d" % n, align_bytes=64) for n in range(6)]

        def widen(n, lo, hi):
            c = chunks[n][1]
            for k in range(lo, hi):
                cols = slice(P * k, P * (k + 1))
                nc.scalar.activation(
                    out=xw[n][:, cols], in_=xb[c][:, cols].bitcast(E4M3), func=ACT.Copy, scale=xs[:, c, k : k + 1]
                )

        def turn(n, h, eng):
            tp = psum.tile([P, 2, 2, P], F32, name="tp", tag="tp", bufs=2)
            pairs = (xw[n] if n < 2 else xw[n][:]).bitcast(F32)
            for i in range(2):
                for u in range(2):
                    c0 = 256 * (2 * h + i)
                    nc.tensor.transpose(tp[:, i, u, :], pairs[:, c0 + u : c0 + 256 : 2], ident[:])
            dst = xg[n][:].bitcast(F32)[:, 512 * h : 512 * (h + 1)].rearrange("p (i r u) -> p i r u", i=2, u=2)
            src = tp[:].rearrange("p i u r -> p i r u")
            if eng == "v":
                nc.vector.tensor_copy(out=dst, in_=src)
            else:
                nc.scalar.copy(out=dst, in_=src)

        def turn_tile(n, i, eng):
            tp = psum.tile([P, 2, P], F32, name="tpt", tag="tp", bufs=2)
            pairs = (xw[n] if n < 2 else xw[n][:]).bitcast(F32)
            for u in range(2):
                nc.tensor.transpose(tp[:, u, :], pairs[:, 256 * i + u : 256 * (i + 1) : 2], ident[:])
            dst = xg[n][:].bitcast(F32)[:, 256 * i : 256 * (i + 1)].rearrange("p (r u) -> p r u", u=2)
            src = tp[:].rearrange("p u r -> p r u")
            if eng == "v":
                nc.vector.tensor_copy(out=dst, in_=src)
            else:
                nc.scalar.copy(out=dst, in_=src)

        def quantize(n):
            nc.vector.quantize_mx(out=xc[n][:].bitcast(E4M3X4), scales=xcs[n][:], in_=xg[n][:])

        pooled = {
            "q": keep.tile([P, VT, NQ], F32, name="pooled_q", align_bytes=64),
            "d": keep.tile([P, VT, ND], F32, name="pooled_d", align_bytes=64),
        }
        banks = {}

        def scores(n, vt):
            side = 0 if chunks[n][0] == "q" else 1
            width = P * tiles_of[n]
            mm = psum.tile([P, 512], F32, name="mm", tag="mm", bufs=6)
            nc.tensor.matmul_mx(
                out=mm[:, :width],
                lhsT=ww[side][:, 2 * P * vt : 2 * P * (vt + 1)].bitcast(E2M1X4),
                lhsT_scale=ws[side][:, P * vt : P * (vt + 1)],
                rhs=xc[n][:].bitcast(E4M3X4),
                rhs_scale=xcs[n][:],
                start=True,
                stop=True,
            )
            banks[n, vt] = mm

        def pool(n, vt):
            kind, c = chunks[n]
            width = P * tiles_of[n]
            mm = banks.pop((n, vt))
            nc.vector.tensor_reduce(
                out=pooled[kind][:, vt, 64 * c : 64 * (c + 1)],
                in_=mm[:, :width].rearrange("p (i d l) -> p d i l", i=tiles_of[n], l=2),
                axis=AX.XY,
                op=ALU.max,
            )

        vcols = keep.tile([P, 24], F32, name="vcols", align_bytes=64)
        nb = keep.tile([P, VT], F32, name="nb", align_bytes=64)
        b1 = keep.tile([P, VT], F32, name="b1", align_bytes=64)
        gneg = keep.tile([P, 2 * VT], F32, name="gneg", align_bytes=64)
        vrows_f = keep.tile([P, 2 * P], F32, name="vrows_f", align_bytes=64)

        def vector_columns():
            tp = psum.tile([P, 2, P], F32, name="tpv", tag="tp", bufs=2)
            for g in range(2):
                nc.tensor.transpose(tp[:, g, :], vrows_f[:, P * g : P * (g + 1)], ident[:])
            nc.scalar.copy(
                out=vcols[:].rearrange("p (v g j) -> p v g j", v=3, g=2),
                in_=tp[:, :, :12].rearrange("p g (v j) -> p v g j", v=3),
            )

        def vector_constants():
            eng = nc.vector
            eng.tensor_scalar(out=nb[:], in0=vcols[:, 0:VT], scalar1=-1.0, scalar2=0.0, op0=ALU.mult, op1=ALU.add)
            eng.tensor_scalar(out=b1[:], in0=vcols[:, 0:VT], scalar1=1.0, scalar2=1.0, op0=ALU.mult, op1=ALU.add)
            for k, count in enumerate((NQ, ND)):
                eng.tensor_scalar(
                    out=gneg[:, VT * k : VT * (k + 1)],
                    in0=vcols[:, VT + VT * k : 2 * VT + VT * k],
                    scalar1=-1.0 / count,
                    scalar2=0.0,
                    op0=ALU.mult,
                    op1=ALU.add,
                )

        logs = {
            "q": keep.tile([P, VT, NQ], F32, name="logs_q", align_bytes=64),
            "d": keep.tile([P, VT, ND], F32, name="logs_d", align_bytes=64),
        }
        sums_q = keep.tile([P, VT], F32, name="sums_q", align_bytes=64)
        sums_d = [keep.tile([P, VT], F32, name="sums_d%d" % k, align_bytes=64) for k in range(2)]
        off_q = keep.tile([P, VT], F32, name="off_q", align_bytes=64)
        off_a = keep.tile([P, VT], F32, name="off_a", align_bytes=64)
        off_s = keep.tile([P, VT], F32, name="off_s", align_bytes=64)
        off_g = keep.tile([P, VT], F32, name="off_g", align_bytes=64)
        off_v = keep.tile([P, VT], F32, name="off_v", align_bytes=64)
        cg = {
            "q": keep.tile([P, 2, NQ, 4], BF16, name="cg_q", align_bytes=64),
            "d": [keep.tile([P, ND, 4], BF16, name="cg_d%d" % g, align_bytes=64) for g in range(2)],
        }
        cc = {
            "q": keep.tile([P, 2, NQ], U32, name="cc_q", align_bytes=64),
            "d": keep.tile([P, 2, ND], U32, name="cc_d", align_bytes=64),
        }
        ccs = {
            "q": keep.tile([P, 2, NQ], U8, name="ccs_q", align_bytes=64),
            "d": keep.tile([P, 2, ND], U8, name="ccs_d", align_bytes=64),
        }

        def clip(eng, kind, vt, lo, hi):
            x = pooled[kind][:, vt, lo:hi]
            eng.tensor_scalar(out=x, in0=x, scalar1=BIG, scalar2=nb[:, vt : vt + 1], op0=ALU.min, op1=ALU.max)

        def relu(kind, vt, lo, hi):
            x = pooled[kind][:, vt, lo:hi]
            nc.scalar.activation(out=x, in_=x, func=ACT.Relu, bias=vcols[:, vt : vt + 1])

        def ln(kind, vt, lo, hi, acc, clipped):
            nc.scalar.activation(
                out=logs[kind][:, vt, lo:hi],
                in_=pooled[kind][:, vt, lo:hi],
                func=ACT.Ln,
                bias=(b1[:, vt : vt + 1] if clipped else ones[:]),
                accum_out=acc[:, vt : vt + 1],
            )

        def gain(kind, vt):
            k = (8 if kind == "q" else 16) + vt
            return vcols[:, k : k + 1]

        cu = keep.tile([P, 4, ND], BF16, name="cu", align_bytes=64)

        def slot(kind, g, j):
            if kind == "q":
                return cg["q"][:, g, :, j]
            return cu[:, j, :] if g == 1 and 1 else cg["d"][g][:, :, j]

        def interleave(lo, hi):
            nc.vector.tensor_copy(out=cg["d"][1][:, lo:hi, :], in_=cu[:, :, lo:hi].rearrange("p j d -> p d j"))

        def centre(eng, kind, vt, off):
            g, j = vt // 4, vt % 4
            if eng == "s":
                nc.scalar.activation(
                    out=slot(kind, g, j), in_=logs[kind][:, vt, :], func=ACT.Identity, scale=gain(kind, vt), bias=off[:, vt : vt + 1]
                )
            else:
                (nc.vector if eng == "v" else nc.gpsimd).tensor_scalar(
                    out=slot(kind, g, j),
                    in0=logs[kind][:, vt, :],
                    scalar1=gain(kind, vt),
                    scalar2=off[:, vt : vt + 1],
                    op0=ALU.mult,
                    op1=ALU.add,
                )

        def quantize_queries():
            nc.vector.quantize_mx(
                out=cc["q"][:].rearrange("p g n -> p (g n)").bitcast(E4M3X4),
                scales=ccs["q"][:].rearrange("p g n -> p (g n)"),
                in_=cg["q"][:].rearrange("p g n j -> p (g n j)"),
            )

        def quantize_docs(g, lo, hi):
            nc.vector.quantize_mx(
                out=cc["d"][:, g, lo:hi].bitcast(E4M3X4),
                scales=ccs["d"][:, g, lo:hi],
                in_=cg["d"][g][:, lo:hi, :].rearrange("p d j -> p (d j)"),
            )

        idle = keep.tile([P, 512], BF16, name="idle", align_bytes=64)
        nc.vector.memset(idle[:], 0.0)
        wake = psum.tile([P, 512], F32, name="mm", tag="mm", bufs=6)
        for k in range(4):
            nc.tensor.matmul(wake[:], lhsT=idle[:, :P], rhs=idle[:], start=True, stop=True)

        turn_tile(0, 0, "v")
        turn_tile(0, 1, "s")
        permute(0, 0, nc.vector)
        quantize(0)
        permute(0, 1, nc.vector)
        if -1 < 0:
            turn_tile(1, 0, "v")
            turn_tile(1, 1, "v")
        widen(2, 0, 16)

        order = [(n, vt) for n in range(4) for vt in range(VT)]
        last = (0, 1, 2, 3, 4, 5, 6, 7)
        LEAD = 2
        order += [(4, vt) for vt in last[:LEAD]]
        for k, vt in enumerate(last):
            if k + LEAD < VT:
                order.append((4, last[k + LEAD]))
            order.append((5, vt))
        AHEAD = 3
        GROUP = 2
        pools = [order[k + GROUP - 1 - m] for k in range(0, len(order) - GROUP, GROUP) for m in range(GROUP)]
        pools += order[len(pools):]
        SPLIT = 128
        VECTOR = (6, 7)
        GPS = (0, 1, 4)
        seen = set()

        def query_logs(lo, hi):
            for k in range(lo, hi):
                if 1 == 2:
                    relu("q", k, 0, NQ)
                ln("q", k, 0, NQ, sums_q, 1 != 2)
            for k in range(lo, hi):
                if k % 4 == 3:
                    cols = slice(k - 3, k + 1)
                    nc.gpsimd.tensor_tensor(out=off_q[:, cols], in0=sums_q[:, cols], in1=gneg[:, cols], op=ALU.mult)

        def query_centres(lo, hi):
            for m in range(lo, hi):
                centre("g" if m < 8 else "s", "q", m, off_q)

        def early(lo, hi):
            for k in range(lo, hi):
                if k < 0:
                    clip(nc.gpsimd, "d", k, 0, SPLIT)
                elif k < 0:
                    clip(nc.vector, "d", k, 0, SPLIT)
                else:
                    relu("d", k, 0, SPLIT)
            for k in range(lo, hi):
                ln("d", k, 0, SPLIT, sums_d[0], k < 0)
            for k in range(lo, hi):
                if k not in VECTOR + GPS and not 0:
                    nc.scalar.activation(out=off_a[:, k : k + 1], in_=sums_d[0][:, k : k + 1], func=ACT.Copy, scale=gneg[:, VT + k : VT + k + 1])

        def offset(k):
            col = slice(k, k + 1)
            dcol = gneg[:, VT + k : VT + k + 1]
            if k in VECTOR or k in GPS or 0:
                eng, dst = (nc.vector, off_v) if k in VECTOR else (nc.gpsimd, off_g)
                if SPLIT == 0:
                    eng.tensor_scalar(out=dst[:, col], in0=sums_d[1][:, col], scalar1=dcol, scalar2=0.0, op0=ALU.mult, op1=ALU.add)
                else:
                    eng.tensor_scalar(
                        out=dst[:, col], in0=sums_d[1][:, col], scalar1=sums_d[0][:, col], scalar2=dcol, op0=ALU.add, op1=ALU.mult
                    )
            elif SPLIT == 0:
                nc.scalar.activation(out=off_s[:, col], in_=sums_d[1][:, col], func=ACT.Copy, scale=dcol)
            else:
                nc.scalar.activation(
                    out=off_s[:, col], in_=sums_d[1][:, col], func=ACT.Identity, scale=dcol, bias=off_a[:, col]
                )

        def final_centre(k):
            if k in VECTOR:
                centre("v", "d", k, off_v)
            elif k in GPS:
                centre("g", "d", k, off_g)
            else:
                centre("s", "d", k, off_g if 0 else off_s)

        late = []
        for i in range(AHEAD):
            scores(*order[i])
        for i, (n, vt) in enumerate(pools):
            if i + AHEAD < len(order):
                scores(*order[i + AHEAD])
            pool(n, vt)
            seen.add((n, vt))
            if i == 5:
                permute(1, 0, nc.gpsimd)
            if i == 9:
                permute(1, 1, nc.gpsimd)
            if i == -1:
                turn_tile(1, 0, "v")
                turn_tile(1, 1, "v")
                widen(2, 16, 16)
            if i == 2:
                quantize(1)
            if i == 3:
                nc.vector.tensor_copy(out=vrows_f[:], in_=vrows[:])
            if i == 2:
                turn(2, 0, "s")
                turn(2, 1, "s")
            if i == 4:
                vector_columns()
                if "vector" == "gpsimd":
                    vector_constants()
                widen(3, 0, 16)
            if 1 == 1 and 10 <= i < 18:
                clip(nc.vector, "q", pools[i - 2][1], 0, NQ)
            if 1 == 0 and i == max(16, 4):
                for k in range(VT):
                    clip(nc.gpsimd, "q", pools[8 + k][1], 0, NQ)
            if i == 7 and "vector" == "vector":
                vector_constants()
            if i == 11:
                quantize(2)
            if i == 12:
                turn(3, 0, "s")
                turn(3, 1, "s")
                widen(4, 0, 16)
            if i == 18:
                query_logs(0, 4)
                query_centres(0, 4)
            if i == 15:
                quantize(3)
            if i == 20:
                turn(4, 0, "s")
                turn(4, 1, "s")
                query_logs(4, 4)
                query_centres(4, 4)
                widen(5, 0, 16)
            if i == 24:
                quantize(4)
            if i == 26:
                turn(5, 0, "s")
                turn(5, 1, "s")
            if i == 26 + 1:
                query_logs(4, 8)
                query_centres(4, 8)
            if i == 30:
                quantize(5)
            if i == 32 and SPLIT > 0:
                early(0, VT)
            if n >= 4 and vt < 7 and (4, vt) in seen and (5, vt) in seen:
                if 0 == 1:
                    for k in late:
                        offset(k)
                if vt < 0:
                    clip(nc.gpsimd, "d", vt, SPLIT, ND)
                elif vt < 0:
                    clip(nc.vector, "d", vt, SPLIT, ND)
                if 0 == 0:
                    for k in late:
                        offset(k)
                if vt >= 0:
                    relu("d", vt, SPLIT, ND)
                for k in late:
                    final_centre(k)
                ln("d", vt, SPLIT, ND, sums_d[1], vt < 0)
                late = [vt]
            if i == 41:
                quantize_queries()
            if i == 47:
                quantize_docs(0, 0, ND)
        if 1:
            for k in late:
                if k not in VECTOR:
                    offset(k)
                    final_centre(k)
            late = [k for k in late if k in VECTOR]
        relu("d", 7, SPLIT, ND)
        ln("d", 7, SPLIT, ND, sums_d[1], False)
        if 47 == 48:
            quantize_docs(0, 0, ND)
        for k in late:
            offset(k)
            final_centre(k)
        offset(7)
        final_centre(7)
        if 47 == 49:
            quantize_docs(0, 0, ND)
        outs = [psum.tile([P, 512], F32, name="mm", tag="mm", bufs=6) for h in range(2)]
        if 1:
            for h in range(2):
                interleave(P * h, P * (h + 1))
        for g in range(2):
            for h in range(2):
                cols = slice(P * h, P * (h + 1))
                if g == 1:
                    quantize_docs(1, P * h, P * (h + 1))
                nc.tensor.matmul_mx(
                    out=outs[h][:, :P],
                    lhsT=cc["q"][:, g, :].bitcast(E4M3X4),
                    lhsT_scale=ccs["q"][:, g, :],
                    rhs=cc["d"][:, g, cols].bitcast(E4M3X4),
                    rhs_scale=ccs["d"][:, g, cols],
                    start=(g == 0),
                    stop=(g == 1),
                )
        res = [keep.tile([P, P], F32, name="res%d" % h, align_bytes=64) for h in range(2)]
        nc.scalar.copy(out=res[0][:], in_=outs[0][:, :P])
        nc.scalar.dma_start(out=out[:, :P], in_=res[0][:])
        nc.vector.tensor_copy(out=res[1][:], in_=outs[1][:, :P])
        nc.sync.dma_start(out=out[:, P:], in_=res[1][:])
